import numpy as np, ml_dtypes
CORES = [6,15,38,47]
N = 4
BF = ml_dtypes.bfloat16
def gentries(a):
    return np.ascontiguousarray(a.reshape(8, 16, -1).transpose(0, 2, 1)).reshape(8, -1)
def gtable(e):
    e = np.asarray(e); return np.ascontiguousarray(e.reshape(8, -1, 16).transpose(0, 2, 1)).reshape(128, -1).astype(np.int32)
V, RO, HOP = 1024, 3, 1
W = N * V
def rings(o, cut):
    t = np.arange(W); c = cut.copy(); c[0] = True
    first = np.maximum.accumulate(np.where(c, t, 0)); nt = np.where(np.append(c[1:], True), first, t + 1)
    nx = np.empty(W, np.int64); pv = np.empty(W, np.int64); nx[o] = o[nt]; pv[o[nt]] = o
    return nx, pv
def walk(rng, n, step):
    w = np.add.accumulate(rng.integers(-step, step + 1, (16, n)), axis=1) + rng.integers(0, 256, (16, 1))
    return np.abs((w + 255) % 510 - 255)
def curve(rng, o, step, off, slide, share):
    h = W // 2; a = walk(rng, h, step); t = np.arange(h)
    xs = np.empty((16, W), np.int64); xs[:, o[:h]] = a; xs[:, o[h:]] = np.clip(a + rng.integers(-off, off + 1, (16, h)), 0, 255)
    cut = rng.random(W) < share
    if share >= 0: cut[h] = True; cut[0:16:3] = True
    nx, pv = rings(o, cut); s = rng.integers(-slide, slide + 1, (2, h)); p = np.empty(W, np.int64)
    p[o[:h]] = o[h + (t + s[0]) % h]; p[o[h:]] = o[(t + s[1]) % h]
    return xs, nx, pv, p
def odd(rng, o, nx, pv, p):
    m = rng.random(W)
    p = np.where(m < 0.03, rng.integers(0, W, W), np.where(m < 0.05, np.arange(W), np.where(m < 0.07, nx, np.where(m < 0.09, pv, p))))
    p[o[0:15:3]] = nx[o[0:15:3]]; p[o[1:15:3]] = pv[o[1:15:3]]
    return p
def links(a):
    return np.stack([gtable(a.reshape(8, N, V)[:, q]) for q in range(N)])
def pack(gs, th):
    xs, nx, pv, p = [np.stack(a) for a in zip(*gs)]
    return {"x": np.ascontiguousarray(xs.reshape(8, 16, N, V).transpose(2, 0, 1, 3)).reshape(N, 128, V).astype(np.int32),
            "nxt": links(nx), "prv": links(pv), "ptn": links(p),
            "th": np.tile(np.repeat(np.asarray(th), 16)[None, :, None], (N, 1, 1)).astype(np.int32)}
def setup_inputs(rng):
    gs, th = [], []
    for g in range(8):
        off = int(rng.integers(4, 13)); step = int(rng.integers(off, 2 * off + 1)); o = rng.permutation(W)
        xs, nx, pv, p = curve(rng, o, step, off, RO, 0.02)
        gs.append((xs, nx, pv, odd(rng, o, nx, pv, p))); th.append(int(rng.integers(4 * off * off, 9 * off * off)))
    return pack(gs, th)
def setup_inputs_ties(rng):
    gs, th = [], []; w = np.arange(W)
    for g in range(8):
        o = rng.permutation(W)
        if g == 6: o = np.ascontiguousarray(w.reshape(N, 2, V // 2).transpose(1, 0, 2)).reshape(-1)
        if g == 7: o = w
        q = int(rng.integers(1, 5)); xs, nx, pv, p = curve(rng, o, 4, 0, 1, -1.0 if g == 5 else 0.02)
        sort = rng.integers(0, 3, W) if g > 1 else np.zeros(W, np.int64)
        u = rng.integers(0, 250, (16, 1)); lo = np.arange(16)[:, None] < 8
        xs = u + q * np.where(sort == 1, lo, np.where(sort == 2, ~lo, False)).astype(np.int64)
        gs.append((xs, nx, pv, p)); th.append((1, 0, 8 * q * q, 8 * q * q + 1, 16 * q * q, 16 * q * q + 1, 8 * q * q, 8 * q * q + 1)[g])
    return pack(gs, th)
def setup_inputs_loops(rng):
    gs, th = [], []; ra, rb, rc = [int(v) for v in rng.permutation(N)[:3]]; w = np.arange(W).reshape(N, V); k = V // 2; c = W - 2 * V; b = W - V
    for g in range(8):
        out = [q for q in range(N) if q != rb and q != rc and (g < 7 or q != ra)]
        few = w[ra] if g == 7 else w[ra][:0]
        o = np.concatenate([rng.permutation(w[out].reshape(-1)), rng.permutation(few), rng.permutation(w[rc]), rng.permutation(w[rb])])
        m = len(out) * V; h = m // 2; t = np.arange(h); j = np.arange(c - m) % 6
        xs = np.empty((16, W), np.int64); xs[:, o] = walk(rng, W, 6)
        xs[:, o[h:m]] = np.clip(xs[:, o[:h]] + rng.integers(-4, 5, (16, h)), 0, 255)
        xs[:, o[c + k:b]] = np.clip(xs[:, o[c:c + k]] + rng.integers(-4, 5, (16, k)), 0, 255)
        cut = rng.random(W) < (1.0, -1.0, 0.5, 0.3, 0.4, 0.05, 0.02, 0.3)[g]
        if g != 1: cut[h] = True
        cut[m] = True; cut[m:c] = (j == 0) | (j == 3) | (j == 5); cut[c:b] = True; cut[b] = True
        if g == 6: cut[1:16] = False
        nx, pv = rings(o, cut); s = rng.integers(-1, 2, (2, h)); p = np.empty(W, np.int64)
        p[o[:h]] = o[h + (t + s[0]) % h]; p[o[h:m]] = o[(t + s[1]) % h]
        i = o[m:c]; u = rng.integers(0, 3, c - m); p[i] = np.where(u == 0, i, np.where(u == 1, nx[i], pv[i]))
        p[o[c:c + k]] = o[c + k:b]; p[o[c + k:b]] = o[c:c + k]; p[o[b:]] = o[rng.integers(0, m, V)]
        if 2 <= g <= 4:
            i = o[0:m:2]; p[i] = np.where(rng.random(h) < 0.7, nx[i], p[i])
            i = o[1:m:2]; p[i] = np.where(rng.random(h) < 0.7, pv[i], p[i])
        if g == 5: p = ra * V + rng.integers(0, V, W)
        if g == 6:
            u = rng.integers(60, 196, (16, 1)); xs = u + rng.integers(-40, 41, (16, W))
            xs[:, o[np.array([5, 20])]] = u; xs[:, o[np.array([3, 4, 6, 7])]] = np.where(u < 128, 255, 0)
            p = np.full(W, o[5], np.int64); p[o[5]] = o[20]
        if g == 7:
            i = o[:m]; p[i] = np.where(rng.random(m) < 0.75, i, p[i])
        gs.append((xs, nx, pv, p)); th.append(10000 if g == 6 else int(rng.integers(300, 4000)))
    return pack(gs, th)
def setup_inputs_ends(rng):
    gs, th = [], []; h = W // 2
    for g in range(8):
        r = 1 + rng.permutation(W - 2); o = np.concatenate([np.array([0]), r[:h - 1], np.array([W - 1]), r[h - 1:]])
        xs, nx, pv, p = curve(rng, o, 4, 0, 0, 0.02)
        if g == 0: p[o[3:15:3]] = nx[o[3:15:3]]; p[o[4:15:3]] = pv[o[4:15:3]]
        xs = 255 * rng.integers(0, 2, (16, W))
        if g == 1:
            nx, pv = rings(o, np.arange(W) % 4 == 0); y = 255 * rng.integers(0, 2, (16, W // 4, 2)); s = rng.integers(0, 3, W)
            xs[:, o] = np.concatenate([y, 255 - y], axis=2).reshape(16, W); p = np.where(s == 0, nx, np.where(s == 1, pv, nx[nx]))
        if g in (2, 3, 7):
            u = 255 * rng.integers(0, 2, (16, 1)); xs[:, o[:h]] = u; xs[:, o[h:]] = 255 - u
        if g == 7: xs[14] = 100; xs[15] = 100 + rng.integers(0, 2, W)
        gs.append((xs, nx, pv, p)); th.append((2 ** 20, 2 ** 20, 1040400, 1040401, 520200, 0, 1, 14 * 255 * 255 + 1)[g])
    return pack(gs, th)
def setup_inputs_near(rng):
    gs, th = [], []; h = W // 2; back = int(rng.integers(0, 2))
    for g in range(8):
        r = np.stack([q * V + rng.permutation(V) for q in range(N)])
        o = np.concatenate([np.ascontiguousarray(r[:, :V // 2].T).reshape(-1), np.ascontiguousarray(np.roll(r[:, V // 2:], N // 2, axis=0).T).reshape(-1)])
        off = int(rng.integers(2, 6)); a = walk(rng, h, 16 * off)
        xs = np.empty((16, W), np.int64); xs[:, o[:h]] = a; xs[:, o[h:]] = np.clip(a + rng.integers(-off, off + 1, (16, h)), 0, 255)
        cut = (rng.random(W) < 0.04) & (np.arange(W) % N == 0); cut[h] = True
        nx, pv = rings(o, cut); mate = np.empty(W, np.int64); mate[o[:h]] = o[h:]; mate[o[h:]] = o[:h]
        gs.append((xs, nx, pv, pv[mate] if back else nx[mate])); th.append(int(rng.integers(17 * off * off, 40 * off * off)))
    return pack(gs, th)
def setup_inputs_spread(rng):
    gs, th = [], []
    for g in range(8):
        o = rng.permutation(W); xs, nx, pv, p = curve(rng, o, int(rng.integers(2, 40)), int(rng.integers(0, 30)), RO, 0.02)
        xs = np.where(rng.random(W) < 0.1, rng.integers(0, 256, (16, W)), xs >> rng.integers(0, 7, (16, 1)))
        gs.append((xs, nx, pv, odd(rng, o, nx, pv, p))); th.append(int(2.0 ** (20 * rng.random())))
    return pack(gs, th)
def joined(a):
    return np.ascontiguousarray(np.stack([gentries(b) for b in a]).transpose(1, 0, 2)).reshape(8, W).astype(np.int64)
def check_inputs(d):
    bad = []
    for k, hi in (("x", 255), ("nxt", W - 1), ("prv", W - 1), ("ptn", W - 1), ("th", 2 ** 20)):
        if np.min(d[k]) < 0 or np.max(d[k]) > hi: bad.append("range of " + k)
    t = d["th"].reshape(N, 8, 16)
    if np.any(t != t[:1, :, :1]): bad.append("th alike on all ranks and in a group")
    if "range of nxt" not in bad and "range of prv" not in bad:
        if np.any(np.take_along_axis(joined(d["prv"]), joined(d["nxt"]), 1) != np.arange(W)[None, :]): bad.append("prv is the inverse of nxt")
    return bad
def at(a, i):
    return np.take_along_axis(a, i, 1)
def points(a, i):
    return np.take_along_axis(a, i[:, None, :], 2)
def reference(x, nxt, prv, ptn, th):
    z = np.ascontiguousarray(x.astype(np.int64).reshape(N, 8, 16, V).transpose(1, 2, 0, 3)).reshape(8, 16, W)
    nx = joined(nxt); pv = joined(prv); p = joined(ptn); t = th[0].astype(np.int64).reshape(8, 16)[:, :1]
    me = np.arange(W)[None, :]
    for rnd in range(RO):
        a = at(nx, p); b = at(pv, p)
        c = np.stack([p, a, b] + ([at(nx, a), at(pv, b)] if HOP == 2 else []))
        d = np.stack([np.add.reduce((z - points(z, k)) ** 2, axis=1) for k in c])
        d = np.where((c == me) | (c == nx) | (c == pv), 2 ** 21, d)
        k = np.argmin(d, axis=0)[None]
        p = np.take_along_axis(c, k, 0)[0]; e = np.take_along_axis(d, k, 0)[0]
        swap = (at(p, p) == me) & (e < t)
        nx, pv = np.where(swap, at(nx, p), nx), np.where(at(swap, pv), at(p, pv), pv)
        z = (2 * z + points(z, nx) + points(z, pv)) >> 2
    return {"yx": np.ascontiguousarray(z.reshape(8, 16, N, V).transpose(2, 0, 1, 3)).reshape(N, 128, V).astype(np.float32),
            "yn": links(nx).astype(np.float32), "yv": links(pv).astype(np.float32), "yp": links(p).astype(np.float32)}

@@ -1,0 +1,451 @@
+from concourse.mybir import AluOpType as ALU, ActivationFunctionType as ACT
+
+F32, F16, BF, I32, U16 = "float32", "float16", "bfloat16", "int32", "uint16"
+SCRATCH = {
+    "xi": ("sbuf", [128, 4, 256], I32), "li": ("sbuf", [128, 192], I32), "thi": ("sbuf", [128, 4], I32),
+    "zero": ("sbuf", [128, 512], F32), "lz": ("sbuf", [128, 448], F16),
+    "snd": ("sbuf", [128, 4, 304], F16), "lnd": ("sbuf", [128, 4, 304], F16),
+    "iS": ("sbuf", [128, 64], F32), "iR": ("sbuf", [128, 128], F32), "iP": ("sbuf", [128, 192], F32),
+    "z16": ("sbuf", [128, 512], F16), "zb": ("sbuf", [128, 128], BF), "pi": ("sbuf", [128, 8], I32),
+    "mX": ("sbuf", [128, 2048], F16), "mO": ("sbuf", [128, 144], F16), "mN": ("sbuf", [128, 128], F16),
+    "mH": ("sbuf", [128, 128], BF), "mE": ("sbuf", [128, 128], BF), "mQ": ("sbuf", [128, 128], F32),
+    "mS": ("sbuf", [128, 128], F16), "mR": ("sbuf", [128, 512], F16), "mP": ("sbuf", [128, 768], F16),
+    "mB": ("sbuf", [128, 512], F16), "mF": ("sbuf", [128, 768], F16), "mW": ("sbuf", [128, 768], F16),
+    "mZ": ("sbuf", [128, 432], F16), "mD": ("sbuf", [128, 8], F32), "mK": ("sbuf", [128, 8], F32),
+    "mG": ("sbuf", [128, 128], F32), "ZB": ("sbuf", [128, 4, 17, 8], F32), "cn": ("sbuf", [128, 64], BF),
+    "mI": ("sbuf", [128, 128], F16), "mJ": ("sbuf", [128, 64], F16), "col": ("sbuf", [128, 16], F32),
+    "FL": ("sbuf", [128, 320], BF), "MK": ("sbuf", [128, 1024], BF), "id16": ("sbuf", [128, 64], F16),
+    "vi": ("sbuf", [128, 128], I32),
+    "X": ("sbuf", [128, 4096], F32), "TB": ("sbuf", [128, 4096], F32),
+    "xo": ("sbuf", [128, 1024], F32), "own": ("sbuf", [128, 1024], F32), "t1": ("sbuf", [128, 1024], F32),
+    "S": ("sbuf", [128, 1024], F16), "D": ("sbuf", [128, 3072], BF), "SQ": ("sbuf", [128, 3072], F32),
+    "GA": ("sbuf", [128, 1024], F16), "GB": ("sbuf", [128, 1024], F16), "GF": ("sbuf", [128, 1024], F32),
+    "L": ("sbuf", [128, 3, 64], F16), "q16": ("sbuf", [128, 64], F16), "CH": ("sbuf", [128, 768], F32),
+    "off": ("sbuf", [128, 576], U16), "sm": ("sbuf", [128, 64 * 24], F32),
+    "lf": ("sbuf", [128, 4, 2, 48], F16), "yl": ("sbuf", [128, 192], F32), "c15": ("sbuf", [128, 16], F16),
+    "sx": ("sbuf", [128, 4, 304], F16), "lx": ("sbuf", [128, 4, 304], F16), "ox": ("sbuf", [128, 4, 256], F32),
+}
+for _b in range(8):
+    SCRATCH["P%d" % _b] = ("psum", [128, 512], F32)
+SEMAPHORES = (["c_v", "c_a", "c_pe", "c_g", "sent", "d_li", "d_th", "d_out"] + ["d_x%d" % i for i in range(4)]
+              + ["d_t%d" % i for i in range(9)] + ["a%d_%d" % (i, j) for i in range(2) for j in range(4)])
+
+M0 = float(2 ** 23 + 1)
+WQ = 0.25 + 2.0 ** -12
+BQ = 2.0 ** 23 - 0.5
+DS = 2.0 ** -23
+RO = 3
+PARTS = (["lz", "mS", "T0", "T1", "T2", "mR", "mP", "mX", "mB", "mF", "mW", "ms", "Ln", "Lv", "Lp", "SQ0", "SQ1", "SQ2", "GF", "MK", "lf"]
+         + ["snd%d" % i for i in range(4)] + ["lnd%d" % i for i in range(4)])
+
+
+def rank_program(g, core, T, topo):
+    rank = T.rank_of(core)
+    if rank is None:
+        return
+    Q = {"v": g.vector, "a": g.scalar, "pe": g.tensor, "g": g, "s": g.sync}
+    total, seen, state = {}, {}, {}
+
+    def wait(e, tok):
+        if seen.get((e, tok[0]), 0) < tok[1]:
+            seen[(e, tok[0])] = tok[1]
+            Q[e].wait_ge(T.sem[tok[0]], tok[1])
+
+    def deps(e, reads, writes):
+        for k in reads:
+            st = state.setdefault(k, {"w": None, "r": {}})
+            if st["w"]:
+                wait(e, st["w"])
+            if k[0] == "P":
+                for t in st["r"].values():
+                    if t[2] != e:
+                        wait(e, t)
+        for k in writes:
+            st = state.setdefault(k, {"w": None, "r": {}})
+            for t in [st["w"]] + list(st["r"].values()):
+                if t and (t[2] != e or not (e == "pe" or (k in PARTS and not st["r"]))):
+                    wait(e, t)
+
+    def mark(tok, reads, writes):
+        for k in reads:
+            state[k]["r"][tok[0]] = tok
+        for k in writes:
+            state[k] = {"w": tok, "r": {}}
+
+    def op(e, fn, reads, writes):
+        deps(e, reads, writes)
+        s = "c_" + e
+        total[s] = total.get(s, 0) + 1
+        fn().then_inc(T.sem[s], 1)
+        mark((s, total[s], e), reads, writes)
+
+    def dmas(e, sem, pairs, reads, writes):
+        deps(e, reads, writes)
+        for o, i in pairs:
+            total[sem] = total.get(sem, 0) + 16
+            Q[e].dma_start(o, i).then_inc(T.sem[sem], 16)
+        mark((sem, total[sem], "dma"), reads, writes)
+
+    def mm(groups, reads, writes):
+        def fn():
+            last = None
+            for out, terms in groups:
+                for n, (a, b) in enumerate(terms):
+                    last = g.tensor.matmul(out, a, b, n == 0, n == len(terms) - 1)
+            return last
+        op("pe", fn, reads, writes)
+
+    def tt(o, a, b, alu, reads, writes):
+        op("v", lambda: g.vector.tensor_tensor(o, a, b, alu), reads, writes)
+
+    def ts(o, a, s1, op0, reads, writes, s2=None, op1=None):
+        if op1 is None:
+            op("v", lambda: g.vector.tensor_scalar(o, a, s1, None, op0), reads, writes)
+        else:
+            op("v", lambda: g.vector.tensor_scalar(o, a, s1, s2, op0, op1), reads, writes)
+
+    def cp(o, a, reads, writes):
+        op("v", lambda: g.vector.tensor_copy(o, a), reads, writes)
+
+    def act(o, a, reads, writes, func=ACT.Identity, **kw):
+        op("a", lambda: g.scalar.activation(o, a, func, **kw), reads, writes)
+
+    def iota(o, pat, base, cm, key):
+        op("g", lambda: g.iota(o, pat, base, cm, allow_small_or_imprecise_dtypes=True), [], [key])
+
+    def dots(o, src, skey, pat, base, val, key, alu=ALU.not_equal, cm=-1):
+        op("g", lambda: g.affine_select(o, src, pat, alu, val, base, cm), [skey], [key])
+
+    def send(phase, d, dst, src, key):
+        deps("g", [key], [])
+        rid, pid = topo.addr(T.cores[d])[:2]
+        total["sent"] = total.get("sent", 0) + len(topo.engines(core, T.cores[d]))
+        g.remote_dma(dst, src, T.sem["a%d_%d" % (phase, rank)], T.sem["sent"], pid, rid, topo.mask(core, T.cores[d]))
+
+    def arrives(phase, src, key):
+        s = "a%d_%d" % (phase, src)
+        total[s] = len(topo.engines(T.cores[src], core))
+        state[key] = {"w": (s, total[s], "rem"), "r": {}}
+
+    slots = {}
+
+    def sm(name, n=1):
+        if name not in slots:
+            slots[name] = len(slots)
+        return T.sm[:, 64 * slots[name]:64 * (slots[name] + n)]
+
+    for name in ("idc", "ab", "ab1", "ab2"):
+        sm(name)
+    OP, OB, OA, ON, OV, OQ, OU, OI, OL = [64 * i for i in range(9)]
+
+    def off(c, a=0, b=64):
+        return T.off[:, c + a:c + b]
+
+    P = [T["P%d" % b] for b in range(8)]
+    XK = ["X%d" % b for b in range(8)]
+    TK = ["T0", "T1", "T2"]
+    NX, PV, PT = T.L[:, 0, :], T.L[:, 1, :], T.L[:, 2, :]
+
+    def far(d):
+        a, b = topo.chip(core), topo.chip(T.cores[d])
+        return 2 if topo.mates(a, b) else 1 if topo.same_plane(a, b) else 0
+    peers = sorted([d for d in range(4) if d != rank], key=far)
+
+    dmas("s", "d_li", [(T.li[:, 0:64], T.nxt[:]), (T.li[:, 64:128], T.prv[:]), (T.li[:, 128:192], T.ptn[:])], [], ["li"])
+    for n, d in enumerate(peers + [rank]):
+        dmas("a" if n % 2 == 0 else "s", "d_x%d" % d, [(T.xi[:, d, :], T.x[32 * d:32 * d + 32, :])], [], ["xi%d" % d])
+    dmas("s", "d_th", [(T.thi[16 * k:16 * k + 16, 0:1], T.th[32 * rank + 16 * (k // 4):32 * rank + 16 * (k // 4) + 16, :])
+                       for k in range(8)], [], ["thi"])
+
+    iota(T.iS[:], [[32, 4], [1, 16]], 0, -1, "iS")
+    iota(T.iR[:], [[64, 2], [0, 4], [4, 16]], 0, -1, "iR")
+    iota(T.iP[:], [[64, 3], [1000, 4], [4, 16]], 0, -1, "iP")
+    iota(T.sm[:, 0:64], [[1, 64]], -2048, 64, "idc")
+    iota(T.col[:, 8:9], [[1, 1]], 0, 1, "pf")
+    op("v", lambda: g.vector.memset(T.zero[:], 0.0), [], ["zero"])
+    cp(T.lz[:], T.zero[:, 0:448], ["zero"], ["lz0"])
+    for h in range(2):
+        ts(T.mS[:, 64 * h:64 * h + 64], T.iS[:], -16.0 * h, ALU.is_equal, ["iS"], ["mS"])
+    cp(T.z16[:], T.zero[:], ["zero"], ["z16"])
+    op("v", lambda: g.vector.memset(T.zb[:], 0.0), [], ["zb"])
+    op("v", lambda: g.vector.memset(T.mD[:], DS), [], ["mD"])
+    for b in range(8):
+        act(T.TB[:, 512 * b:512 * b + 512], T.zero[:], ["zero"], TK, func=ACT.Copy)
+
+    for t in range(3):
+        ts(T.lz[:, 64 + 128 * t:128 + 128 * t], T.li[:, 64 * t:64 * t + 64], -2048.0, ALU.add, ["li", "lz0"], ["lz"])
+    for n, d in enumerate(peers + [rank]):
+        mm([(P[n][:, 16 * t:16 * t + 16],
+             [(T.lz[:, 128 * t + 64 - 64 * h:128 * t + 192 - 64 * h], T.mS[:, 64 * h + 16 * d:64 * h + 16 * d + 16]) for h in range(2)])
+            for t in range(3)], ["lz", "mS"], ["P%d" % n])
+    for n, d in enumerate(peers + [rank]):
+        buf, key = (T.lnd, "lnd%d" % d) if d == rank else (T.snd, "snd%d" % d)
+        cp(buf[:, d, 0:256], T.xi[:, d, :], ["xi%d" % d], [key])
+        cp(buf[:, d, 256:304], P[n][:, 0:48], ["P%d" % n], [key])
+        if d != rank:
+            send(0, d, T.lnd[:, rank, :], T.snd[:, d, :], key)
+            arrives(0, d, "lnd%d" % d)
+    ts(T.mO[:], T.zero[:, 0:144], 1.0, ALU.add, ["zero"], ["mO"])
+    ts(T.c15[:], T.zero[:, 0:16], 1.5, ALU.add, ["zero"], ["c15"])
+    ZP = [[16, 9], [1000, 16]]
+    dots(T.mI[:], T.z16[:, 0:128], "z16", [[1, 128]], 0, 1.0, "mI")
+    dots(T.mN[:], T.z16[:, 0:128], "z16", [[1, 128]], 0, -1.0, "mN")
+    for j in range(4):
+        dots(T.mX[:, 512 * j:512 * j + 512], T.z16[:], "z16", [[1, 4], [16, 8], [0, 16]], 4 * j, 1.0, "mX")
+    dots(T.mD[:], T.mD[:], "mD", [[16, 8]], 15, 0.0, "mD", ALU.is_ge)
+    dots(T.mD[:], T.mD[:], "mD", [[-16, 8]], 0, 0.0, "mD", ALU.is_ge, 1)
+    dots(T.mG[:], T.zero[:, 0:128], "zero", [[1, 2], [2, 64]], 0, 1.0, "mG")
+    for t in range(2):
+        dots(T.mZ[:, 144 * t:144 * t + 144], T.z16[:, 0:144], "z16", ZP, t - 15000, 1.0, "mZ%d" % t)
+    dots(T.mE[:], T.zb[:], "zb", [[1, 128]], 0, 0.125, "mE")
+    dots(T.mH[:], T.zb[:], "zb", [[1, 128]], 0, 0.5, "mH")
+    dots(T.mZ[:, 288:432], T.z16[:, 0:144], "z16", ZP, 2 - 15000, 1.0, "mZ2")
+    dots(T.mO[:], T.mO[:], "mO", ZP, 15 - 15000, 0.0, "mO", ALU.is_ge)
+    dots(T.mO[:], T.mO[:], "mO", [[-16, 9], [-1000, 16]], 15000, 0.0, "mO", ALU.is_ge, 1)
+    dots(T.mK[:], T.zero[:, 0:8], "zero", [[16, 8]], 2, 4096.0, "mK")
+    dots(T.mK[:], T.mK[:], "mK", [[16, 8]], 0, 1.0, "mK")
+    dots(T.mQ[:], T.zero[:, 0:128], "zero", [[1, 128]], 0, -4096.0, "mQ")
+    for j in range(4):
+        dots(T.mB[:, 128 * j:128 * j + 128], T.z16[:, 0:128], "z16", [[64, 2], [0, 4], [1, 16]], 16 * j, 1.0, "mB")
+    for j in range(4):
+        for m, w in (("mF", 1.0), ("mW", WQ)):
+            dots(T[m][:, 192 * j:192 * j + 192], T.z16[:, 0:192], "z16", [[64, 3], [1, 16], [1000, 4]], 16 * j - 3000, w, m)
+    dots(T.mJ[:], T.z16[:, 0:64], "z16", [[1, 64]], 0, 1.0, "mJ")
+    dots(T.mJ[:], T.mJ[:], "mJ", [[1, 64]], 64, 1.0, "mJ")
+    for j in range(4):
+        ts(T.mR[:, 128 * j:128 * j + 128], T.iR[:], -1.0 * j, ALU.is_equal, ["iR"], ["mR"])
+    for j in range(4):
+        ts(T.mP[:, 192 * j:192 * j + 192], T.iP[:], 3000.0 - j, ALU.is_equal, ["iP"], ["mP"])
+    ts(T.sm[64:128, 0:64], T.sm[64:128, 0:64], -4096.0, ALU.add, ["idc"], ["idc"])
+    ts(off(OI), sm("idc"), 2048.0, ALU.add, ["idc"], ["oI"])
+    cp(T.id16[:], sm("idc"), ["idc"], ["id16"])
+    cp(T.pi[:, 0:1], T.col[:, 8:9], ["pf"], ["pi0"])
+    ts(T.col[:, 4:5], T.col[:, 8:9], 64.0, ALU.is_lt, ["pf"], ["ms"])
+    ts(T.col[:, 5:6], T.col[:, 8:9], 64.0, ALU.is_ge, ["pf"], ["ms"])
+    ts(T.pi[:, 4:5], T.pi[:, 0:1], 15, ALU.bitwise_and, ["pi0"], ["pi1"])
+    ts(T.col[:, 6:7], T.pi[:, 4:5], -256.0, ALU.mult, ["pi1"], ["rb"], 2048.0 - 127.5, ALU.add)
+    ts(T.col[:, 0:1], T.thi[:, 0:1], DS, ALU.mult, ["thi"], ["th"])
+    op("v", lambda: g.vector.memset(T.ZB[:], 0.0), [], ["ZB0", "ZB1", "ZB2", "ZB3"])
+
+    def first_block(n, q):
+        for hb in range(2):
+            b = (2 * n + hb) % 4
+            mm([(P[b][:, 256 * jj:256 * jj + 256],
+                 [(T.mR[:, 128 * (2 * hb + jj):128 * (2 * hb + jj) + 128], T.lnd[:, q, 0:256])]) for jj in range(2)],
+               ["mR", "lnd%d" % q], ["P%d" % b])
+            o = T.X[:, 1024 * q + 512 * hb:1024 * q + 512 * hb + 512]
+            if hb == 0 and n > 0:
+                ts(o, P[b][:], M0, ALU.add, ["P%d" % b], [XK[2 * q + hb]])
+            else:
+                act(o, P[b][:], ["P%d" % b], [XK[2 * q + hb]], bias=M0)
+
+    def to_table(items):
+        for src, key, row, sem in items:
+            c = 256 * (row % 2)
+            mm([(P[6][:, c + 64 * j:c + 64 * j + 64], [(T.mR[:, 128 * j:128 * j + 128], src)]) for j in range(4)], ["mR", key], ["P6"])
+        r0, n = items[0][2], len(items)
+        act(T.CH[:, 256 * r0:256 * (r0 + n)], P[6][:, 256 * (r0 % 2):256 * (r0 % 2 + n)], ["P6"],
+            ["CH%d" % i[2] for i in items], func=ACT.Copy)
+        for src, key, row, sem in items:
+            dmas("s", sem, [(T.TB[row::16, :], T.CH[:, 256 * row:256 * row + 256])], ["CH%d" % row], [TK[row]])
+
+    def first_lists(n, q):
+        def fn():
+            ins = None
+            for j in range(4):
+                ins = g.tensor.matmul(P[4 + j][:, 0:48], T.mP[:, 192 * j + 48 - 16 * q:192 * j + 176 - 16 * q], T.lnd[:, q, 256:304],
+                                      n == 0, n == 3)
+            return ins
+        op("pe", fn, ["mP", "lnd%d" % q], ["P4", "P5", "P6", "P7"])
+
+    def flags():
+        mm([(P[6][:, 64 * n:64 * n + 64], [(T.mI[:], PT), (T.mN[:], o)]) for n, o in enumerate((T.id16[:], NX, PV))],
+           ["mI", "mN", "id16", "Ln", "Lv", "Lp"], ["P6"])
+        act(sm("ab", 3), P[6][:, 0:192], ["P6"], ["ab"], func=ACT.Abs)
+        act(T.FL[:, 0:192], sm("ab", 3), ["ab"], ["FL"], func=ACT.Relu, scale=-1.0, bias=1.0)
+
+    for n, q in enumerate([rank] + peers):
+        first_lists(n, q)
+        if n == 3:
+            for j in range(4):
+                cp(T.L[:, :, 16 * j:16 * j + 16], P[4 + j][:, 0:48], ["P%d" % (4 + j)], ["Ln", "Lv", "Lp"])
+        first_block(n, q)
+    to_table([(NX, "Ln", 0, "d_t0"), (PV, "Lv", 1, "d_t1")])
+    ts(off(OP), PT, 2048.0, ALU.add, ["Lp"], ["oP"])
+    cp(T.xo[:, 0:512], T.X[:, 0:4096].indirect(off(OI, 0, 32)), XK + ["oI"], ["xo0"])
+    act(T.xo[:, 512:1024], T.X[:, 0:4096].indirect(off(OI, 32, 64)), XK + ["oI"], ["xo1"], func=ACT.Copy)
+    flags()
+
+    def pick(out, z, zc, src):
+        return (out, [(z[:, zc + 15 - r:zc + 143 - r], src[:, r:1024:16]) for r in range(16)])
+
+    def neighbours():
+        cp(T.GA[:], T.TB[:, 0:4096].indirect(off(OP)), TK + ["oP"], ["GA"])
+        mm([pick(P[7][:, 64:128], T.mZ, 0, T.GA), pick(P[7][:, 0:64], T.mZ, 144, T.GA)], ["mZ0", "mZ1", "GA"], ["P7"])
+
+    def distance(n, oc, okey, cuts):
+        for a, b in cuts:
+            tt(T.D[:, 1024 * n + a:1024 * n + b], T.X[:, 0:4096].indirect(off(oc, a // 16, b // 16)), T.xo[:, a:b], ALU.subtract,
+               XK + [okey, "xo0", "xo1"], ["D%d_%d" % (n, a)])
+            act(T.SQ[:, 1024 * n + a:1024 * n + b], T.D[:, 1024 * n + a:1024 * n + b], ["D%d_%d" % (n, a)], ["SQ%d" % n], func=ACT.Square)
+
+    def turn(bank, w, src, c0, key):
+        mm([(P[bank][:, 128 + r:192:8], [(src[:, c0 + r:c0 + 1024:8], T[w][:])]) for r in range(8)], [w, key], ["P%d" % bank])
+
+    def space(n, bank, e="a"):
+        if e == "a":
+            act(T.ZB[:, n, 1::2, :], P[bank][:, 128:192], ["P%d" % bank], ["ZB%d" % n], func=ACT.Copy)
+        else:
+            cp(T.ZB[:, n, 1::2, :], P[bank][:, 128:192], ["P%d" % bank], ["ZB%d" % n])
+
+    def turn_back(n, more):
+        return [(T.ZB[:, n, 1 - h:17 - h, :], T.mG[:, 64 * h:64 * h + 64]) for h in range(2)] + more
+
+    def distance_out(n, bank, m, fl):
+        mm([(P[bank][:, 0:64], turn_back(n, [(T[m][:], T.FL[:, 64 * f:64 * f + 64]) for f in fl]))],
+           ["mG", m, "ZB%d" % n, "FL"] + (["f"] if n else []), ["P%d" % bank])
+
+    def low_offsets():
+        ts(T.vi[:, 0:64], PV, 2048.0, ALU.add, ["Lv"], ["vi0"])
+        ts(T.vi[:, 64:128], T.vi[:, 0:64], 255, ALU.bitwise_and, ["vi0"], ["vi1"])
+        cp(off(OL), T.vi[:, 64:128], ["vi1"], ["oL"])
+
+    def spread(h, bank):
+        mm([(P[bank][:, r:512:16], [(T.mX[:, 128 * r:128 * r + 128], T.L[:, 1, 32 * h:32 * h + 32])]) for r in range(16)],
+           ["mX", "Lv"], ["P%d" % bank])
+
+    def spread_out(h, bank):
+        act(T.GF[:, 512 * h:512 * h + 512], P[bank][:], ["P%d" % bank, "rb"], ["GF"], func=ACT.Abs, bias=T.col[:, 6:7])
+
+    def mask(h):
+        act(T.MK[:, 512 * h:512 * h + 512], T.GF[:, 512 * h:512 * h + 512], ["GF"], ["MK"], func=ACT.Sigmoid, scale=-1000.0, bias=128000.0)
+
+    fine = [(0, 512), (512, 768), (768, 1024)]
+    for rnd in range(RO):
+        last = rnd == RO - 1
+        if rnd == 0:
+            spread(0, 3)
+            spread(1, 4)
+        distance(0, OP, "oP", fine)
+        if rnd == 0:
+            spread_out(0, 3)
+        turn(0, "mD", T.SQ, 0, "SQ0")
+        space(0, 0)
+        if rnd == 0:
+            spread_out(1, 4)
+            mask(0)
+            neighbours()
+            low_offsets()
+            tt(sm("pid"), PT, sm("idc"), ALU.subtract, ["Lp", "idc"], ["pid"])
+        distance_out(0, 0, "mE", (0, 1, 2))
+        ts(T.off[:, OB:OB + 128], P[7][:, 0:128], 2048.0, ALU.add, ["P7"], ["oBA"])
+        tt(T.FL[:, 192:320], P[7][:, 0:128], T.L[:, 0:2, :], ALU.is_equal, ["P7", "Ln", "Lv"], ["f"])
+        distance(1, OA, "oBA", [(0, 512), (512, 1024)])
+        act(sm("e0"), P[0][:, 0:64], ["P0"], ["e0"], func=ACT.Copy)
+        turn(5, "mD", T.SQ, 1024, "SQ1")
+        distance(2, OB, "oBA", fine)
+        space(1, 5, "v")
+        distance_out(1, 5, "mH", (0, 2, 4))
+        turn(1, "mD", T.SQ, 2048, "SQ2")
+        space(2, 1)
+        distance_out(2, 1, "mH", (0, 1, 3))
+        mask(1)
+        tt(sm("ap"), P[7][:, 64:128], PT, ALU.subtract, ["P7", "Lp"], ["ap"])
+        tt(sm("bid"), P[7][:, 0:64], sm("idc"), ALU.subtract, ["P7", "idc"], ["bid"])
+        tt(sm("c"), P[5][:, 0:64], sm("e0"), ALU.is_lt, ["P5", "e0"], ["c"])
+        tt(sm("m01"), P[5][:, 0:64], sm("e0"), ALU.min, ["P5", "e0"], ["m01"])
+        tt(sm("t"), sm("c"), sm("ap"), ALU.mult, ["c", "ap"], ["t"])
+        ts(sm("v"), sm("m01"), T.col[:, 0:1], ALU.is_lt, ["m01", "th"], ["v"])
+        tt(sm("dq"), sm("t"), sm("pid"), ALU.add, ["t", "pid"], ["dq"])
+        ts(sm("mt"), sm("m01"), T.col[:, 0:1], ALU.min, ["m01", "th"], ["mt"])
+        tt(sm("t2"), sm("v"), sm("dq"), ALU.mult, ["v", "dq"], ["t2"])
+        tt(sm("dbp"), sm("bid"), sm("dq"), ALU.subtract, ["bid", "dq"], ["dbp"])
+        tt(sm("dbq"), sm("bid"), sm("t2"), ALU.subtract, ["bid", "t2"], ["dbq"])
+        tt(sm("q01"), sm("t2"), sm("idc"), ALU.add, ["t2", "idc"], ["q01"])
+        tt(sm("u1"), P[1][:, 0:64], sm("mt"), ALU.is_lt, ["P1", "mt"], ["u1"])
+        tt(sm("u2"), sm("u1"), sm("dbq"), ALU.mult, ["u1", "dbq"], ["u2"])
+        tt(T.q16[:], sm("u2"), sm("q01"), ALU.add, ["u2", "q01"], ["q16"])
+        to_table([(T.q16[:], "q16", 2, "d_t%d" % (2 + 3 * rnd))])
+        act(T.own[:], T.xo[:], ["xo0", "xo1"], ["own"], scale=2.0, bias=4.0 - 4.0 * M0)
+        tt(sm("u3"), P[1][:, 0:64], sm("m01"), ALU.is_lt, ["P1", "m01"], ["u3"])
+        ts(off(OQ), T.q16[:], 2048.0, ALU.add, ["q16"], ["oQ"])
+        tt(sm("u4"), sm("u3"), sm("dbp"), ALU.mult, ["u3", "dbp"], ["u4"])
+        tt(T.GA[:], T.CH[:, 512:768].indirect(off(OL)), T.MK[:], ALU.mult, ["CH2", "oL", "MK"], ["GA"])
+        mm([pick(P[2][:, 0:64], T.mO, 0, T.GA)], ["mO", "GA"], ["P2"])
+        tt(sm("pid"), sm("u4"), sm("dq"), ALU.add, ["u4", "dq"], ["pid"])
+        tt(PT, sm("pid"), sm("idc"), ALU.add, ["pid", "idc"], ["Lp"])
+        ts(off(OU), P[2][:, 0:64], 2048.0, ALU.add, ["P2"], ["oU"])
+        cp(T.GB[:], T.TB[:, 0:4096].indirect(off(OU)), TK + ["oU"], ["GB"])
+        act(T.GF[:], T.TB[:, 0:4096].indirect(off(OQ)), TK + ["oQ"], ["GF"], func=ACT.Copy)
+        mm([pick(P[4][:, 0:64], T.mZ, 288, T.GB)], ["mZ2", "GB"], ["P4"])
+        turn(3, "mK", T.GF, 0, "GF")
+        space(3, 3)
+        mm([(P[3][:, 0:64], turn_back(3, [(T.mQ[:], sm("idc"))])),
+            (P[3][:, 64:128], turn_back(3, [(T.mQ[:], sm("idc")), (T.mN[:], NX)]))], ["mG", "mQ", "mN", "idc", "Ln", "ZB3"], ["P3"])
+        act(sm("ab"), P[3][:, 0:64], ["P3"], ["ab"], func=ACT.Abs, bias=0.5)
+        act(T.cn[:], sm("ab"), ["ab"], ["cn"], func=ACT.Sigmoid, scale=-1000.0, bias=2048000.0)
+        tt(sm("du"), P[2][:, 0:64], PV, ALU.subtract, ["P2", "Lv"], ["du"])
+        if not last:
+            ts(off(OP), PT, 2048.0, ALU.add, ["Lp"], ["oP"])
+        tt(sm("u2"), P[4][:, 0:64], PV, ALU.is_equal, ["P4", "Lv"], ["u2"])
+        tt(sm("u3"), sm("u2"), sm("du"), ALU.mult, ["u2", "du"], ["u3"])
+        tt(PV, sm("u3"), PV, ALU.add, ["u3", "Lv"], ["Lv"])
+        ts(off(OV), PV, 2048.0, ALU.add, ["Lv"], ["oV"])
+        if not last:
+            spread(0, 0)
+            spread(1, 1)
+            spread_out(0, 0)
+        tt(T.t1[:], T.X[:, 0:4096].indirect(off(OV)), T.own[:], ALU.add, XK + ["oV", "own"], ["t1"])
+        tt(sm("u4"), P[3][:, 64:128], T.cn[:], ALU.mult, ["P3", "cn"], ["u4"])
+        tt(NX, sm("u4"), NX, ALU.add, ["u4", "Ln"], ["Ln"])
+        ts(off(ON), NX, 2048.0, ALU.add, ["Ln"], ["oN"])
+        if not last:
+            to_table([(NX, "Ln", 0, "d_t%d" % (3 + 3 * rnd)), (PV, "Lv", 1, "d_t%d" % (4 + 3 * rnd))])
+            spread_out(1, 1)
+        else:
+            for n, d in enumerate(peers + [rank]):
+                mm([(P[4 + n][:, 256 + t:304:3],
+                     [(T.mF[:, 192 * d + 3 - j:192 * d + 131 - j], T.L[:, t, 16 * j:16 * j + 16]) for j in range(4)]
+                     + [(T.mI[:], T.c15[:])]) for t in range(3)], ["mF", "mI", "c15", "Ln", "Lv", "Lp"], ["P%d" % (4 + n)])
+        for h in range(2):
+            tt(T.S[:, 512 * h:512 * h + 512], T.X[:, 0:4096].indirect(off(ON, 32 * h, 32 * h + 32)), T.t1[:, 512 * h:512 * h + 512],
+               ALU.add, XK + ["oN", "t1"], ["S%d" % h])
+            if not last:
+                mm([(P[h][:], [(T.mI[:], T.S[:, 512 * h:512 * h + 512])])], ["mI", "S%d" % h], ["P%d" % h])
+                act(T.xo[:, 512 * h:512 * h + 512], P[h][:], ["P%d" % h], ["xo%d" % h], scale=WQ, bias=BQ)
+        if not last:
+            low_offsets()
+            for b in range(8):
+                k = (2 + b) % 6
+                mm([(P[k][:, 64 * r:64 * r + 64], [(T.mB[:, 128 * (b // 2):128 * (b // 2) + 128], T.S[:, 8 * (b % 2) + r:1024:16])])
+                    for r in range(8)], ["mB", "S0", "S1"], ["P%d" % k])
+                o = T.X[:, 512 * b:512 * b + 512]
+                if b in (0, 2, 4):
+                    ts(o, P[k][:], WQ, ALU.mult, ["P%d" % k], [XK[b]], BQ, ALU.add)
+                else:
+                    act(o, P[k][:], ["P%d" % k], [XK[b]], scale=WQ, bias=BQ)
+            flags()
+            mask(0)
+            neighbours()
+
+    for n, d in enumerate(peers + [rank]):
+        k = 4 + n
+        mm([(P[k][:, 64 * r:64 * r + 64],
+             [(T.mW[:, 192 * d + 3 - j:192 * d + 131 - j], T.S[:, 4 * j + r:1024:16]) for j in range(4)]) for r in range(4)],
+           ["mW", "S0", "S1"], ["P%d" % k])
+        buf, key = (T.lx, "lx%d" % d) if d == rank else (T.sx, "sx%d" % d)
+        ts(buf[:, d, :], P[k][:, 0:304], BQ, ALU.add, ["P%d" % k], [key], M0, ALU.subtract)
+        if d != rank:
+            send(1, d, T.lx[:, rank, :], T.sx[:, d, :], key)
+            arrives(1, d, "lx%d" % d)
+    for n, d in enumerate([rank] + peers):
+        if n == 3:
+            for s in range(2):
+                ts(T.lf[:, :, s, :], T.lx[:, :, 256:304], T.col[:, 4 + s:5 + s], ALU.mult, ["ms"] + ["lx%d" % i for i in range(4)], ["lf"])
+        cp(T.ox[:, d, :], T.lx[:, d, 0:256], ["lx%d" % d], ["ox%d" % d])
+        dmas("s", "d_out", [(T.yx[32 * d:32 * d + 32, :], T.ox[:, d, :])], ["ox%d" % d], [])
+    mm([(P[0][:, 64 * t:64 * t + 64], [(T.lf[:, :, :, t:48:3], T.mJ[:])]) for t in range(3)], ["mJ", "lf"], ["P0"])
+    act(T.yl[:], P[0][:, 0:192], ["P0"], ["yl"], bias=2048.0)
+    dmas("a", "d_out", [(T.yn[:], T.yl[:, 0:64]), (T.yv[:], T.yl[:, 64:128]), (T.yp[:], T.yl[:, 128:192])], ["yl"], [])
+    for s, v in total.items():
+        g.wait_ge(T.sem[s], v)

@@ -3,40 +3,42 @@ from concourse.mybir import AluOpType as ALU, ActivationFunctionType as ACT
 F32, F16, BF, I32, U16 = "float32", "float16", "bfloat16", "int32", "uint16"
 SCRATCH = {
     "xi": ("sbuf", [128, 4, 256], I32), "li": ("sbuf", [128, 192], I32), "thi": ("sbuf", [128, 4], I32),
-    "zero": ("sbuf", [128, 512], F32), "lz": ("sbuf", [128, 448], F16),
+    "zb": ("sbuf", [128, 1160], BF), "lz": ("sbuf", [128, 448], F16),
     "snd": ("sbuf", [128, 4, 304], F16), "lnd": ("sbuf", [128, 4, 304], F16),
-    "iS": ("sbuf", [128, 64], F32), "iR": ("sbuf", [128, 128], F32), "iP": ("sbuf", [128, 192], F32),
-    "z16": ("sbuf", [128, 512], F16), "zb": ("sbuf", [128, 128], BF), "pi": ("sbuf", [128, 8], I32),
-    "mX": ("sbuf", [128, 2048], F16), "mO": ("sbuf", [128, 144], F16), "mN": ("sbuf", [128, 128], F16),
-    "mH": ("sbuf", [128, 128], BF), "mE": ("sbuf", [128, 128], BF), "mQ": ("sbuf", [128, 128], F32),
-    "mS": ("sbuf", [128, 128], F16), "mR": ("sbuf", [128, 512], F16), "mP": ("sbuf", [128, 768], F16),
-    "mB": ("sbuf", [128, 512], F16), "mF": ("sbuf", [128, 768], F16), "mW": ("sbuf", [128, 768], F16),
-    "mZ": ("sbuf", [128, 432], F16), "mD": ("sbuf", [128, 8], F32), "mK": ("sbuf", [128, 8], F32),
-    "mG": ("sbuf", [128, 128], F32), "ZB": ("sbuf", [128, 4, 17, 8], F32), "cn": ("sbuf", [128, 64], BF),
-    "mI": ("sbuf", [128, 128], F16), "mJ": ("sbuf", [128, 64], F16), "col": ("sbuf", [128, 16], F32),
-    "FL": ("sbuf", [128, 320], BF), "MK": ("sbuf", [128, 1024], BF), "id16": ("sbuf", [128, 64], F16),
-    "vi": ("sbuf", [128, 128], I32),
-    "X": ("sbuf", [128, 4096], F32), "TB": ("sbuf", [128, 4096], F32),
-    "xo": ("sbuf", [128, 1024], F32), "own": ("sbuf", [128, 1024], F32), "t1": ("sbuf", [128, 1024], F32),
-    "S": ("sbuf", [128, 1024], F16), "D": ("sbuf", [128, 3072], BF), "SQ": ("sbuf", [128, 3072], F32),
-    "GA": ("sbuf", [128, 1024], F16), "GB": ("sbuf", [128, 1024], F16), "GF": ("sbuf", [128, 1024], F32),
-    "L": ("sbuf", [128, 3, 64], F16), "q16": ("sbuf", [128, 64], F16), "CH": ("sbuf", [128, 768], F32),
-    "off": ("sbuf", [128, 576], U16), "sm": ("sbuf", [128, 64 * 24], F32),
-    "lf": ("sbuf", [128, 4, 2, 48], F16), "yl": ("sbuf", [128, 192], F32), "c15": ("sbuf", [128, 16], F16),
+    "iS": ("sbuf", [128, 64], BF), "iR": ("sbuf", [128, 128], BF), "iW": ("sbuf", [128, 128], BF), "iK": ("sbuf", [128, 64], F32),
+    "mX": ("sbuf", [128, 2048], BF), "mO": ("sbuf", [128, 144], BF), "mI": ("sbuf", [128, 6, 128], BF),
+    "mS": ("sbuf", [128, 128], BF), "mR": ("sbuf", [128, 512], BF), "mP": ("sbuf", [128, 128], BF),
+    "mW": ("sbuf", [128, 1088], BF), "mF": ("sbuf", [128, 768], BF), "mZ": ("sbuf", [128, 400], BF), "mB": ("sbuf", [128, 512], BF),
+    "mT": ("sbuf", [128, 80], BF), "mD": ("sbuf", [128, 8], F32), "mG": ("sbuf", [128, 128], BF),
+    "mJ": ("sbuf", [128, 64], BF), "col": ("sbuf", [128, 16], F32), "one": ("sbuf", [128, 128], F32),
+    "pi": ("sbuf", [128, 16], I32), "thT": ("sbuf", [128, 2, 64], F32),
+    "TT": ("sbuf", [128, 145, 8], F16), "FL": ("sbuf", [128, 320], BF), "MK": ("sbuf", [128, 1024], BF),
+    "X0": ("sbuf", [128, 4096], BF), "X1": ("sbuf", [128, 4096], BF), "TB": ("sbuf", [128, 4096], F32),
+    "xo": ("sbuf", [128, 1024], F16), "D": ("sbuf", [128, 3072], F16), "SQ": ("sbuf", [128, 3072], F32),
+    "GN": ("sbuf", [128, 1024], F16), "GU": ("sbuf", [128, 1024], F16), "GB": ("sbuf", [128, 1024], F16),
+    "GF": ("sbuf", [128, 1024], F16), "G1": ("sbuf", [128, 1024], F16), "G2": ("sbuf", [128, 1024], F16),
+    "GD": ("sbuf", [128, 1024], F16), "AB": ("sbuf", [128, 512], F32), "hi": ("sbuf", [128, 64], F16),
+    "CH": ("sbuf", [128, 768], F32), "off": ("sbuf", [128, 576], U16), "sm": ("sbuf", [128, 64 * 24], F32),
+    "lf": ("sbuf", [128, 3, 4, 2, 16], F16), "yl": ("sbuf", [128, 192], F32),
     "sx": ("sbuf", [128, 4, 304], F16), "lx": ("sbuf", [128, 4, 304], F16), "ox": ("sbuf", [128, 4, 256], F32),
 }
 for _b in range(8):
-    SCRATCH["P%d" % _b] = ("psum", [128, 512], F32)
+    SCRATCH["P%d" % _b] = ("psum", [128, 16, 4, 8], F32)
 SEMAPHORES = (["c_v", "c_a", "c_pe", "c_g", "sent", "d_li", "d_th", "d_out"] + ["d_x%d" % i for i in range(4)]
-              + ["d_t%d" % i for i in range(9)] + ["a%d_%d" % (i, j) for i in range(2) for j in range(4)])
+              + ["d_t%d" % i for i in range(9)] + ["a%d_%d" % (i, j) for i in range(4) for j in range(4)])
 
-M0 = float(2 ** 23 + 1)
-WQ = 0.25 + 2.0 ** -12
-BQ = 2.0 ** 23 - 0.5
+XB = 1280.0
 DS = 2.0 ** -23
 RO = 3
-PARTS = (["lz", "mS", "T0", "T1", "T2", "mR", "mP", "mX", "mB", "mF", "mW", "ms", "Ln", "Lv", "Lp", "SQ0", "SQ1", "SQ2", "GF", "MK", "lf"]
-         + ["snd%d" % i for i in range(4)] + ["lnd%d" % i for i in range(4)])
+SN, SV, SI, SZ, SP, SB, SA, SW = 0, 1, 2, 3, 5, 6, 7, 8
+RV, RN, RW = 0, 1, 2
+PARTS = ["lz", "mS", "T0", "T1", "T2", "sl", "sy", "mX", "mF", "mR", "mW", "mL", "mT", "ms", "lf", "mB"]
+AS = 512
+NV0 = 512
+CUT2 = [(0, 512), (512, 768), (768, 1024)]
+SMOOTH = "g0 p0 p1 s0 g1 s1 C0 c1 g2 X0 s2 g3 x1 h B0 s3 b1 X2 B2 x3 n f B3 B4 B5 B6 b7 t"
+SBANK = (1, 2, 0, 1)
+BBANK = (4, 6, 7, 2, 0, 4, 6, 7)
 
 
 def rank_program(g, core, T, topo):
@@ -53,24 +55,24 @@ def rank_program(g, core, T, topo):
 
     def deps(e, reads, writes):
         for k in reads:
-            st = state.setdefault(k, {"w": None, "r": {}})
-            if st["w"]:
-                wait(e, st["w"])
+            st = state.setdefault(k, {"w": {}, "r": {}})
+            for t in st["w"].values():
+                wait(e, t)
             if k[0] == "P":
                 for t in st["r"].values():
                     if t[2] != e:
                         wait(e, t)
         for k in writes:
-            st = state.setdefault(k, {"w": None, "r": {}})
-            for t in [st["w"]] + list(st["r"].values()):
-                if t and (t[2] != e or not (e == "pe" or (k in PARTS and not st["r"]))):
+            st = state.setdefault(k, {"w": {}, "r": {}})
+            for t in list(st["w"].values()) + list(st["r"].values()):
+                if t[2] != e or not (e == "pe" or (k in PARTS and not st["r"])):
                     wait(e, t)
 
     def mark(tok, reads, writes):
         for k in reads:
             state[k]["r"][tok[0]] = tok
         for k in writes:
-            state[k] = {"w": tok, "r": {}}
+            state[k] = {"w": {tok[0]: tok}, "r": {}}
 
     def op(e, fn, reads, writes):
         deps(e, reads, writes)
@@ -95,6 +97,14 @@ def rank_program(g, core, T, topo):
             return last
         op("pe", fn, reads, writes)
 
+    def acc(terms, reads, bank, start=False, stop=False):
+        def fn():
+            last = None
+            for n, (out, a, b) in enumerate(terms):
+                last = g.tensor.matmul(out, a, b, start and n == 0, stop and n == len(terms) - 1)
+            return last
+        op("pe", fn, reads, ["P%d" % bank])
+
     def tt(o, a, b, alu, reads, writes):
         op("v", lambda: g.vector.tensor_tensor(o, a, b, alu), reads, writes)
 
@@ -107,8 +117,19 @@ def rank_program(g, core, T, topo):
     def cp(o, a, reads, writes):
         op("v", lambda: g.vector.tensor_copy(o, a), reads, writes)
 
-    def act(o, a, reads, writes, func=ACT.Identity, **kw):
+    def fill(o, c, keys):
+        op("v", lambda: g.vector.memset(o, c), [], keys)
+
+    def act(o, a, reads, writes, func=ACT.Copy, **kw):
         op("a", lambda: g.scalar.activation(o, a, func, **kw), reads, writes)
+
+    def move(e, o, a, reads, writes, add=None):
+        if add is None:
+            (cp if e == "v" else act)(o, a, reads, writes)
+        elif e == "v":
+            ts(o, a, add, ALU.add, reads, writes)
+        else:
+            act(o, a, reads, writes, func=ACT.Identity, bias=add)
 
     def iota(o, pat, base, cm, key):
         op("g", lambda: g.iota(o, pat, base, cm, allow_small_or_imprecise_dtypes=True), [], [key])
@@ -116,336 +137,404 @@ def rank_program(g, core, T, topo):
     def dots(o, src, skey, pat, base, val, key, alu=ALU.not_equal, cm=-1):
         op("g", lambda: g.affine_select(o, src, pat, alu, val, base, cm), [skey], [key])
 
-    def send(phase, d, dst, src, key):
-        deps("g", [key], [])
+    def send(phase, d, dst, src, keys, land):
+        deps("g", keys, [])
         rid, pid = topo.addr(T.cores[d])[:2]
         total["sent"] = total.get("sent", 0) + len(topo.engines(core, T.cores[d]))
         g.remote_dma(dst, src, T.sem["a%d_%d" % (phase, rank)], T.sem["sent"], pid, rid, topo.mask(core, T.cores[d]))
-
-    def arrives(phase, src, key):
-        s = "a%d_%d" % (phase, src)
-        total[s] = len(topo.engines(T.cores[src], core))
-        state[key] = {"w": (s, total[s], "rem"), "r": {}}
-
-    slots = {}
-
-    def sm(name, n=1):
-        if name not in slots:
-            slots[name] = len(slots)
-        return T.sm[:, 64 * slots[name]:64 * (slots[name] + n)]
-
-    for name in ("idc", "ab", "ab1", "ab2"):
-        sm(name)
-    OP, OB, OA, ON, OV, OQ, OU, OI, OL = [64 * i for i in range(9)]
-
-    def off(c, a=0, b=64):
-        return T.off[:, c + a:c + b]
-
-    P = [T["P%d" % b] for b in range(8)]
-    XK = ["X%d" % b for b in range(8)]
-    TK = ["T0", "T1", "T2"]
-    NX, PV, PT = T.L[:, 0, :], T.L[:, 1, :], T.L[:, 2, :]
+        s = "a%d_%d" % (phase, d)
+        total[s] = len(topo.engines(T.cores[d], core))
+        state[land] = {"w": {s: (s, total[s], "rem")}, "r": {}}
 
     def far(d):
         a, b = topo.chip(core), topo.chip(T.cores[d])
         return 2 if topo.mates(a, b) else 1 if topo.same_plane(a, b) else 0
     peers = sorted([d for d in range(4) if d != rank], key=far)
 
-    dmas("s", "d_li", [(T.li[:, 0:64], T.nxt[:]), (T.li[:, 64:128], T.prv[:]), (T.li[:, 128:192], T.ptn[:])], [], ["li"])
+    slots = {}
+
+    def sm(name, n=1):
+        if name not in slots:
+            slots[name] = len(slots)
+            for i in range(1, n):
+                slots[name + str(i)] = len(slots)
+        return T.sm[:, 64 * slots[name]:64 * (slots[name] + n)]
+
+    OP, OB, OA, ON, OV, OW, OU, OI, OL = [64 * i for i in range(9)]
+
+    def off(c, a=0, b=64):
+        return T.off[:, c + a:c + b]
+
+    def tf(a, n=1):
+        return T.TT[:, 16 * a + 1:16 * (a + n):2, :]
+
+    P = [T["P%d" % b] for b in range(8)]
+
+    def pc(b, a, n):
+        return P[b][:, a // 32:(a + n) // 32, :, :]
+
+    TK = ["T0", "T1", "T2"]
+    XO = ["xo0", "xo1", "xo2", "xo3"]
+    XT = [T.X0, T.X1, T.X0]
+    XK = [["X%d_%d" % (r % 2, b) for b in range(8)] for r in range(RO)]
+    EYE, NEG, TWO, M256, EIGHTH, HALF = [T.mI[:, i, :] for i in range(6)]
+    TH = T.thT[:, 0, :]
+
     for n, d in enumerate(peers + [rank]):
-        dmas("a" if n % 2 == 0 else "s", "d_x%d" % d, [(T.xi[:, d, :], T.x[32 * d:32 * d + 32, :])], [], ["xi%d" % d])
-    dmas("s", "d_th", [(T.thi[16 * k:16 * k + 16, 0:1], T.th[32 * rank + 16 * (k // 4):32 * rank + 16 * (k // 4) + 16, :])
-                       for k in range(8)], [], ["thi"])
+        dmas("s", "d_x%d" % d, [(T.xi[:, d, :], T.x[32 * d:32 * d + 32, :])], [], ["xi%d" % d])
+        if n == 0:
+            dmas("a", "d_li", [(T.li[:, 0:64], T.nxt[:]), (T.li[:, 64:128], T.prv[:])], [], [])
+            dmas("s", "d_li", [(T.li[:, 128:192], T.ptn[:])], [], ["li"])
+    dmas("s", "d_th", [(T.thi[:, 0:1], T.th[:])], [], ["thi"])
 
     iota(T.iS[:], [[32, 4], [1, 16]], 0, -1, "iS")
     iota(T.iR[:], [[64, 2], [0, 4], [4, 16]], 0, -1, "iR")
-    iota(T.iP[:], [[64, 3], [1000, 4], [4, 16]], 0, -1, "iP")
-    iota(T.sm[:, 0:64], [[1, 64]], -2048, 64, "idc")
-    iota(T.col[:, 8:9], [[1, 1]], 0, 1, "pf")
-    op("v", lambda: g.vector.memset(T.zero[:], 0.0), [], ["zero"])
-    cp(T.lz[:], T.zero[:, 0:448], ["zero"], ["lz0"])
+    iota(T.iW[:], [[1000, 2], [0, 4], [8, 16]], 0, -1, "iW")
+    op("g", lambda: g.iota(T.pi[:, 0:1], [[1, 1]], 0, 1), [], ["pi0"])
+    iota(T.iK[:], [[0, 2], [1, 32]], -2048, 32, "iK")
+    fill(T.zb[:, 0:512], 0.0, ["zb"])
+    cp(T.lz[:], T.zb[:, 0:448], ["zb"], ["lz0"])
     for h in range(2):
         ts(T.mS[:, 64 * h:64 * h + 64], T.iS[:], -16.0 * h, ALU.is_equal, ["iS"], ["mS"])
-    cp(T.z16[:], T.zero[:], ["zero"], ["z16"])
-    op("v", lambda: g.vector.memset(T.zb[:], 0.0), [], ["zb"])
-    op("v", lambda: g.vector.memset(T.mD[:], DS), [], ["mD"])
-    for b in range(8):
-        act(T.TB[:, 512 * b:512 * b + 512], T.zero[:], ["zero"], TK, func=ACT.Copy)
-
-    for t in range(3):
-        ts(T.lz[:, 64 + 128 * t:128 + 128 * t], T.li[:, 64 * t:64 * t + 64], -2048.0, ALU.add, ["li", "lz0"], ["lz"])
-    for n, d in enumerate(peers + [rank]):
-        mm([(P[n][:, 16 * t:16 * t + 16],
-             [(T.lz[:, 128 * t + 64 - 64 * h:128 * t + 192 - 64 * h], T.mS[:, 64 * h + 16 * d:64 * h + 16 * d + 16]) for h in range(2)])
-            for t in range(3)], ["lz", "mS"], ["P%d" % n])
-    for n, d in enumerate(peers + [rank]):
-        buf, key = (T.lnd, "lnd%d" % d) if d == rank else (T.snd, "snd%d" % d)
-        cp(buf[:, d, 0:256], T.xi[:, d, :], ["xi%d" % d], [key])
-        cp(buf[:, d, 256:304], P[n][:, 0:48], ["P%d" % n], [key])
-        if d != rank:
-            send(0, d, T.lnd[:, rank, :], T.snd[:, d, :], key)
-            arrives(0, d, "lnd%d" % d)
-    ts(T.mO[:], T.zero[:, 0:144], 1.0, ALU.add, ["zero"], ["mO"])
-    ts(T.c15[:], T.zero[:, 0:16], 1.5, ALU.add, ["zero"], ["c15"])
-    ZP = [[16, 9], [1000, 16]]
-    dots(T.mI[:], T.z16[:, 0:128], "z16", [[1, 128]], 0, 1.0, "mI")
-    dots(T.mN[:], T.z16[:, 0:128], "z16", [[1, 128]], 0, -1.0, "mN")
-    for j in range(4):
-        dots(T.mX[:, 512 * j:512 * j + 512], T.z16[:], "z16", [[1, 4], [16, 8], [0, 16]], 4 * j, 1.0, "mX")
-    dots(T.mD[:], T.mD[:], "mD", [[16, 8]], 15, 0.0, "mD", ALU.is_ge)
-    dots(T.mD[:], T.mD[:], "mD", [[-16, 8]], 0, 0.0, "mD", ALU.is_ge, 1)
-    dots(T.mG[:], T.zero[:, 0:128], "zero", [[1, 2], [2, 64]], 0, 1.0, "mG")
-    for t in range(2):
-        dots(T.mZ[:, 144 * t:144 * t + 144], T.z16[:, 0:144], "z16", ZP, t - 15000, 1.0, "mZ%d" % t)
-    dots(T.mE[:], T.zb[:], "zb", [[1, 128]], 0, 0.125, "mE")
-    dots(T.mH[:], T.zb[:], "zb", [[1, 128]], 0, 0.5, "mH")
-    dots(T.mZ[:, 288:432], T.z16[:, 0:144], "z16", ZP, 2 - 15000, 1.0, "mZ2")
-    dots(T.mO[:], T.mO[:], "mO", ZP, 15 - 15000, 0.0, "mO", ALU.is_ge)
-    dots(T.mO[:], T.mO[:], "mO", [[-16, 9], [-1000, 16]], 15000, 0.0, "mO", ALU.is_ge, 1)
-    dots(T.mK[:], T.zero[:, 0:8], "zero", [[16, 8]], 2, 4096.0, "mK")
-    dots(T.mK[:], T.mK[:], "mK", [[16, 8]], 0, 1.0, "mK")
-    dots(T.mQ[:], T.zero[:, 0:128], "zero", [[1, 128]], 0, -4096.0, "mQ")
-    for j in range(4):
-        dots(T.mB[:, 128 * j:128 * j + 128], T.z16[:, 0:128], "z16", [[64, 2], [0, 4], [1, 16]], 16 * j, 1.0, "mB")
-    for j in range(4):
-        for m, w in (("mF", 1.0), ("mW", WQ)):
-            dots(T[m][:, 192 * j:192 * j + 192], T.z16[:, 0:192], "z16", [[64, 3], [1, 16], [1000, 4]], 16 * j - 3000, w, m)
-    dots(T.mJ[:], T.z16[:, 0:64], "z16", [[1, 64]], 0, 1.0, "mJ")
-    dots(T.mJ[:], T.mJ[:], "mJ", [[1, 64]], 64, 1.0, "mJ")
+    fill(T.zb[:, 512:1160], 0.0, ["zc"])
+    dots(T.mP[:], T.zb[:, 0:128], "zb", [[64, 2], [1, 2], [2, 32]], 0, 1.0, "mP")
     for j in range(4):
         ts(T.mR[:, 128 * j:128 * j + 128], T.iR[:], -1.0 * j, ALU.is_equal, ["iR"], ["mR"])
+    for b in range(8):
+        act(T.TB[:, 512 * b:512 * b + 512], T.zb[:, 0:512], ["zb"], TK)
+
+    for n, d in enumerate(peers + [rank]):
+        key = ("lnd%d" if d == rank else "snd%d") % d
+        ts(T.snd[:, d, 0:256], T.xi[:, d, :], XB, ALU.add, ["xi%d" % d], [key])
+        if n == 0:
+            send(1, d, T.lnd[:, rank, 0:256], T.snd[:, d, 0:256], [key], "lnd%d" % d)
+            for t in range(3):
+                ts(T.lz[:, 64 + 128 * t:128 + 128 * t], T.li[:, 64 * t:64 * t + 64], -2048.0, ALU.add, ["li", "lz0"], ["lz"])
+            mm([(pc(0, 64 * t, 64), [(T.lz[:, 128 * t + 64 - 64 * h:128 * t + 192 - 64 * h], T.mS[:, 64 * h:64 * h + 64]) for h in range(2)])
+                for t in range(3)], ["lz", "mS"], ["P0"])
+            for t in range(3):
+                cp(T.snd[:, :, 256 + 16 * t:272 + 16 * t], pc(0, 64 * t, 64), ["P0"], ["sl"])
+        elif n < 3:
+            send(1, d, T.lnd[:, rank, :], T.snd[:, d, :], [key, "sl"], "lnd%d" % d)
+        if n == 2:
+            send(0, peers[0], T.lnd[:, rank, 256:304], T.snd[:, peers[0], 256:304], ["sl"], "ll%d" % peers[0])
+
+    def landed(q):
+        return T.snd if q == rank else T.lnd
+
+    cp(T.mW[:, 0:64], T.zb[:, 0:64], ["zb"], ["mW"])
+    for j in range(8):
+        ts(T.mW[:, 64 + 128 * j:192 + 128 * j], T.iW[:], -1.0 * j, ALU.is_equal, ["iW"], ["mW"])
+    cp(T.TT[:], T.zb[:], ["zb", "zc"], ["TT"])
+    dots(T.mG[:], T.zb[:, 0:128], "zb", [[1, 2], [2, 64]], 0, 1.0, "mG")
+    dots(EYE, T.zb[:, 0:128], "zb", [[1, 128]], 0, 1.0, "mI")
+    dots(NEG, T.zb[:, 0:128], "zb", [[1, 128]], 0, -1.0, "mK")
+    for c, pat, row in ((0, [[1, 2]], RV), (16, [[0, 1]], RN), (24, [[1, 2]], RV), (40, [[1000, 2]], RN), (56, [[0, 2]], RW)):
+        dots(T.mT[:, c:c + 8 * pat[0][1]], T.zb[:, 0:8 * pat[0][1]], "zb", pat + [[16, 8]], row, 1.0, "mT")
+    iota(T.mD[:], [[0, 8]], 1, 0, "mD")
+    dots(T.mD[:], T.mD[:], "mD", [[16, 8]], 15, 0.0, "mD", ALU.is_ge)
+    dots(T.mD[:], T.mD[:], "mD", [[-16, 8]], 0, 0.0, "mD", ALU.is_ge, 1)
+    iota(T.thT[:, 1, :], [[16, 2], [0, 32]], 32 * rank, -1, "iT")
+    iota(T.one[:], [[0, 128]], 1, 0, "one")
     for j in range(4):
-        ts(T.mP[:, 192 * j:192 * j + 192], T.iP[:], 3000.0 - j, ALU.is_equal, ["iP"], ["mP"])
-    ts(T.sm[64:128, 0:64], T.sm[64:128, 0:64], -4096.0, ALU.add, ["idc"], ["idc"])
-    ts(off(OI), sm("idc"), 2048.0, ALU.add, ["idc"], ["oI"])
-    cp(T.id16[:], sm("idc"), ["idc"], ["id16"])
-    cp(T.pi[:, 0:1], T.col[:, 8:9], ["pf"], ["pi0"])
-    ts(T.col[:, 4:5], T.col[:, 8:9], 64.0, ALU.is_lt, ["pf"], ["ms"])
-    ts(T.col[:, 5:6], T.col[:, 8:9], 64.0, ALU.is_ge, ["pf"], ["ms"])
+        dots(T.mX[:, 512 * j:512 * j + 512], T.zb[:, 0:512], "zb", [[1, 4], [16, 8], [0, 16]], 4 * j, 1.0, "mX")
+    for j in range(4):
+        dots(T.mB[:, 128 * j:128 * j + 128], T.zb[:, 0:128], "zb", [[64, 2], [0, 4], [1, 16]], 16 * j, 1.0, "mB")
+    for j in range(4):
+        dots(T.mF[:, 192 * j:192 * j + 192], T.zb[:, 0:192], "zb", [[64, 3], [1, 16], [1000, 4]], 16 * j - 3000, 1.0, "mF")
+    dots(T.mZ[:], T.zb[:, 0:400], "zb", [[1, 400]], -65, 1.0, "mZ", cm=-2)
+    dots(T.mJ[:], T.zb[:, 0:64], "zb", [[1, 64]], 0, 1.0, "mJ")
+    dots(T.mJ[:], T.mJ[:], "mJ", [[1, 64]], 64, 1.0, "mJ")
     ts(T.pi[:, 4:5], T.pi[:, 0:1], 15, ALU.bitwise_and, ["pi0"], ["pi1"])
-    ts(T.col[:, 6:7], T.pi[:, 4:5], -256.0, ALU.mult, ["pi1"], ["rb"], 2048.0 - 127.5, ALU.add)
-    ts(T.col[:, 0:1], T.thi[:, 0:1], DS, ALU.mult, ["thi"], ["th"])
-    op("v", lambda: g.vector.memset(T.ZB[:], 0.0), [], ["ZB0", "ZB1", "ZB2", "ZB3"])
+    act(tf(SI), T.iK[:], ["iK", "TT"], ["tI"])
+    move("a", T.col[:, 6:7], T.pi[:, 4:5], ["pi1"], ["rc"], XB)
+
+    def pieces(slot, key, bank):
+        mm([(P[bank][:, j, :, :], [(T.mW[:, 64 + 128 * j - 64 * s:192 + 128 * j - 64 * s], T.TT[:, 16 * slot + 1 + 8 * s:16 * slot + 9 + 8 * s:2, :])
+                                   for s in range(2)]) for j in range(8)], ["mW", key], ["P%d" % bank])
+
+    def table(e, row, bank, sem):
+        move(e, T.CH[:, 256 * row:256 * row + 256], pc(bank, 0, 256), ["P%d" % bank], ["CH%d" % row])
+        dmas("s", sem, [(T.TB[row::16, :], T.CH[:, 256 * row:256 * row + 256])], ["CH%d" % row], [TK[row]])
+
+    def turn(bank, col, n, w, src):
+        return [(P[bank][:, col // 32:(col + 8 * n) // 32, :, r], src[:, r:1024:8], w) for r in range(8)]
+
+    def back(bank, col, slot):
+        return (pc(bank, col, 64), [(T.TT[:, 16 * slot + 1 - h:16 * slot + 17 - h, :], T.mG[:, 64 * h:64 * h + 64]) for h in range(2)])
+
+    def high(bank, col):
+        act(T.hi[:], pc(bank, col, 64), ["P%d" % bank], ["hi"], func=ACT.Identity, scale=1.0 / 256, bias=XB + 8.0 - 127.5 / 256)
+
+    def low():
+        o, terms = back(0, 0, SV)
+        mm([(o, terms + [(M256, T.hi[:])])], ["mG", "mL", "tNV", "hi"], ["P0"])
+
+    def flags_sum():
+        acc([(pc(3, 0, 512), EYE, T.zb[:, 0:512]), (pc(3, 128, 64), NEG, tf(SP)), (pc(3, 192, 128), NEG, tf(SN, 2)), (pc(3, 320, 192), NEG, tf(SN, 3))]
+            + [(pc(3, 320 + 64 * n, 64), EYE, tf(SP)) for n in range(3)], ["mI", "mK", "tNV", "tI", "tP", "zb"], 3, True)
+
+    def n_gather(nv):
+        act(T.GN[:, nv:1024], T.TB[:, 0:4096].indirect(off(OP, nv // 16, 64)), TK + ["oP"], ["GN1"])
+        if nv:
+            cp(T.GN[:, 0:nv], T.TB[:, 0:4096].indirect(off(OP, 0, nv // 16)), TK + ["oP"], ["GN0"])
+
+    def n_turn():
+        acc(turn(3, 0, 40, T.mT[:, 0:40], T.GN), ["mT", "GN0", "GN1"], 3, False, True)
+        act(tf(SB, 2), pc(3, 0, 128), ["P3", "TT"], ["tBA"])
+        mm([back(5, 0, SB), back(5, 64, SA)], ["mG", "tBA"], ["P5"])
+        move("a", T.off[:, OB:OB + 128], pc(5, 0, 128), ["P5"], ["oBA"], 2048.0)
 
     def first_block(n, q):
         for hb in range(2):
-            b = (2 * n + hb) % 4
-            mm([(P[b][:, 256 * jj:256 * jj + 256],
-                 [(T.mR[:, 128 * (2 * hb + jj):128 * (2 * hb + jj) + 128], T.lnd[:, q, 0:256])]) for jj in range(2)],
+            b = 4 + (2 * n + hb) % 4
+            mm([(pc(b, 256 * jj, 256), [(T.mR[:, 128 * (2 * hb + jj):128 * (2 * hb + jj) + 128], landed(q)[:, q, 0:256])]) for jj in range(2)],
                ["mR", "lnd%d" % q], ["P%d" % b])
-            o = T.X[:, 1024 * q + 512 * hb:1024 * q + 512 * hb + 512]
-            if hb == 0 and n > 0:
-                ts(o, P[b][:], M0, ALU.add, ["P%d" % b], [XK[2 * q + hb]])
-            else:
-                act(o, P[b][:], ["P%d" % b], [XK[2 * q + hb]], bias=M0)
+            move("va"[hb], T.X0[:, 1024 * q + 512 * hb:1024 * q + 512 * hb + 512], pc(b, 0, 512), ["P%d" % b], [XK[0][2 * q + hb]], -XB)
 
-    def to_table(items):
-        for src, key, row, sem in items:
-            c = 256 * (row % 2)
-            mm([(P[6][:, c + 64 * j:c + 64 * j + 64], [(T.mR[:, 128 * j:128 * j + 128], src)]) for j in range(4)], ["mR", key], ["P6"])
-        r0, n = items[0][2], len(items)
-        act(T.CH[:, 256 * r0:256 * (r0 + n)], P[6][:, 256 * (r0 % 2):256 * (r0 % 2 + n)], ["P6"],
-            ["CH%d" % i[2] for i in items], func=ACT.Copy)
-        for src, key, row, sem in items:
-            dmas("s", sem, [(T.TB[row::16, :], T.CH[:, 256 * row:256 * row + 256])], ["CH%d" % row], [TK[row]])
+    def first_lists(q, key):
+        mm([(P[2][32 * q:32 * q + 32, s:6:2, 2 * j:2 * j + 2, :], [(T.mP[:, 64 * s + 32 * j:64 * s + 32 * j + 32], landed(q)[:, q, 256:304])])
+            for s in range(2) for j in range(2)], ["mP", key], ["P2"])
 
-    def first_lists(n, q):
-        def fn():
-            ins = None
-            for j in range(4):
-                ins = g.tensor.matmul(P[4 + j][:, 0:48], T.mP[:, 192 * j + 48 - 16 * q:192 * j + 176 - 16 * q], T.lnd[:, q, 256:304],
-                                      n == 0, n == 3)
-            return ins
-        op("pe", fn, ["mP", "lnd%d" % q], ["P4", "P5", "P6", "P7"])
+    def gather_d(rnd, n, oc, okey, a, b):
+        tt(T.D[:, 1024 * n + a:1024 * n + b], XT[rnd][:, 0:4096].indirect(off(oc, a // 16, b // 16)), T.xo[:, a:b], ALU.subtract,
+           XK[rnd] + [okey] + XO, ["D%d_%d" % (n, a)])
 
-    def flags():
-        mm([(P[6][:, 64 * n:64 * n + 64], [(T.mI[:], PT), (T.mN[:], o)]) for n, o in enumerate((T.id16[:], NX, PV))],
-           ["mI", "mN", "id16", "Ln", "Lv", "Lp"], ["P6"])
-        act(sm("ab", 3), P[6][:, 0:192], ["P6"], ["ab"], func=ACT.Abs)
-        act(T.FL[:, 0:192], sm("ab", 3), ["ab"], ["FL"], func=ACT.Relu, scale=-1.0, bias=1.0)
+    def square(n, a, b):
+        act(T.SQ[:, 1024 * n + a:1024 * n + b], T.D[:, 1024 * n + a:1024 * n + b], ["D%d_%d" % (n, a)], ["SQ%d_%d" % (n, a)],
+            func=ACT.Square, bias=XB)
 
-    for n, q in enumerate([rank] + peers):
-        first_lists(n, q)
-        if n == 3:
-            for j in range(4):
-                cp(T.L[:, :, 16 * j:16 * j + 16], P[4 + j][:, 0:48], ["P%d" % (4 + j)], ["Ln", "Lv", "Lp"])
-        first_block(n, q)
-    to_table([(NX, "Ln", 0, "d_t0"), (PV, "Lv", 1, "d_t1")])
-    ts(off(OP), PT, 2048.0, ALU.add, ["Lp"], ["oP"])
-    cp(T.xo[:, 0:512], T.X[:, 0:4096].indirect(off(OI, 0, 32)), XK + ["oI"], ["xo0"])
-    act(T.xo[:, 512:1024], T.X[:, 0:4096].indirect(off(OI, 32, 64)), XK + ["oI"], ["xo1"], func=ACT.Copy)
-    flags()
+    def sums(n, m, fl, keys):
+        acc([(pc(n, 0, 64), m, T.FL[:, 64 * f:64 * f + 64]) for f in fl], ["mL", "FL"], n, True)
+        acc([(P[n][:, 0:2, :, r], T.SQ[:, 1024 * n + r:1024 * n + 1024:8], T.mD[:]) for r in range(8)],
+            ["mE"] + ["SQ%d_%s" % (n, k) for k in keys], n, False, True)
 
-    def pick(out, z, zc, src):
-        return (out, [(z[:, zc + 15 - r:zc + 143 - r], src[:, r:1024:16]) for r in range(16)])
+    def spread(h):
+        mm([(P[6 + h][:, :, r // 8::2, r % 8], [(T.mX[:, 128 * r:128 * r + 128], T.hi[:, 32 * h:32 * h + 32])]) for r in range(16)],
+           ["mX", "hi"], ["P%d" % (6 + h)])
 
-    def neighbours():
-        cp(T.GA[:], T.TB[:, 0:4096].indirect(off(OP)), TK + ["oP"], ["GA"])
-        mm([pick(P[7][:, 64:128], T.mZ, 0, T.GA), pick(P[7][:, 0:64], T.mZ, 144, T.GA)], ["mZ0", "mZ1", "GA"], ["P7"])
-
-    def distance(n, oc, okey, cuts):
-        for a, b in cuts:
-            tt(T.D[:, 1024 * n + a:1024 * n + b], T.X[:, 0:4096].indirect(off(oc, a // 16, b // 16)), T.xo[:, a:b], ALU.subtract,
-               XK + [okey, "xo0", "xo1"], ["D%d_%d" % (n, a)])
-            act(T.SQ[:, 1024 * n + a:1024 * n + b], T.D[:, 1024 * n + a:1024 * n + b], ["D%d_%d" % (n, a)], ["SQ%d" % n], func=ACT.Square)
-
-    def turn(bank, w, src, c0, key):
-        mm([(P[bank][:, 128 + r:192:8], [(src[:, c0 + r:c0 + 1024:8], T[w][:])]) for r in range(8)], [w, key], ["P%d" % bank])
-
-    def space(n, bank, e="a"):
-        if e == "a":
-            act(T.ZB[:, n, 1::2, :], P[bank][:, 128:192], ["P%d" % bank], ["ZB%d" % n], func=ACT.Copy)
+    def mask(h, e):
+        o = T.MK[:, 512 * h:512 * h + 512]
+        if e == "v":
+            ts(o, pc(6 + h, 0, 512), T.col[:, 6:7], ALU.is_equal, ["P%d" % (6 + h), "rc"], ["MK%d" % h])
         else:
-            cp(T.ZB[:, n, 1::2, :], P[bank][:, 128:192], ["P%d" % bank], ["ZB%d" % n])
+            act(T.AB[:], pc(6 + h, 0, 512), ["P%d" % (6 + h), "rc"], ["AB"], func=ACT.Abs, bias=T.col[:, 6:7], scale=-1.0)
+            act(o, T.AB[:], ["AB"], ["MK%d" % h], func=ACT.Relu, scale=-1.0, bias=1.0)
 
-    def turn_back(n, more):
-        return [(T.ZB[:, n, 1 - h:17 - h, :], T.mG[:, 64 * h:64 * h + 64]) for h in range(2)] + more
+    first_block(0, rank)
+    first_block(1, peers[0])
+    cp(T.mO[:], T.zb[:, 0:144], ["zb"], ["mO"])
+    ts(T.col[:, 0:1], T.thi[:, 0:1], DS, ALU.mult, ["thi"], ["th"])
+    first_lists(rank, "sl")
+    first_block(2, peers[1])
+    first_lists(peers[1], "lnd%d" % peers[1])
+    mm([back(1, 0, SI)], ["mG", "tI"], ["P1"])
+    move("a", off(OI), pc(1, 0, 64), ["P1"], ["oI"], 2048.0)
+    first_block(3, peers[2])
+    first_lists(peers[2], "lnd%d" % peers[2])
+    first_lists(peers[0], "ll%d" % peers[0])
+    cp(tf(SN, 2), pc(2, 0, 128), ["P2", "TT"], ["tNV"])
+    pieces(SV, "tNV", 1)
+    pieces(SN, "tNV", 0)
+    act(tf(SP), pc(2, 128, 64), ["P2", "TT"], ["tP"])
+    table("v", RV, 1, "d_t0")
+    table("a", RN, 0, "d_t1")
+    mm([back(4, 0, SP), back(4, 64, SV)], ["mG", "tP", "tNV"], ["P4"])
+    for h in range(2):
+        move("va"[h], T.xo[:, 512 * h:512 * h + 512], T.X0[:, 0:4096].indirect(off(OI, 32 * h, 32 * h + 32)), XK[0] + ["oI"], XO[2 * h:2 * h + 2], XB)
+    ts(off(OP), pc(4, 0, 64), 2048.0, ALU.add, ["P4"], ["oP"])
+    high(4, 64)
+    flags_sum()
 
-    def distance_out(n, bank, m, fl):
-        mm([(P[bank][:, 0:64], turn_back(n, [(T[m][:], T.FL[:, 64 * f:64 * f + 64]) for f in fl]))],
-           ["mG", m, "ZB%d" % n, "FL"] + (["f"] if n else []), ["P%d" % bank])
-
-    def low_offsets():
-        ts(T.vi[:, 0:64], PV, 2048.0, ALU.add, ["Lv"], ["vi0"])
-        ts(T.vi[:, 64:128], T.vi[:, 0:64], 255, ALU.bitwise_and, ["vi0"], ["vi1"])
-        cp(off(OL), T.vi[:, 64:128], ["vi1"], ["oL"])
-
-    def spread(h, bank):
-        mm([(P[bank][:, r:512:16], [(T.mX[:, 128 * r:128 * r + 128], T.L[:, 1, 32 * h:32 * h + 32])]) for r in range(16)],
-           ["mX", "Lv"], ["P%d" % bank])
-
-    def spread_out(h, bank):
-        act(T.GF[:, 512 * h:512 * h + 512], P[bank][:], ["P%d" % bank, "rb"], ["GF"], func=ACT.Abs, bias=T.col[:, 6:7])
-
-    def mask(h):
-        act(T.MK[:, 512 * h:512 * h + 512], T.GF[:, 512 * h:512 * h + 512], ["GF"], ["MK"], func=ACT.Sigmoid, scale=-1000.0, bias=128000.0)
-
-    fine = [(0, 512), (512, 768), (768, 1024)]
     for rnd in range(RO):
         last = rnd == RO - 1
+        X = XT[rnd][:, 0:4096]
+        a0 = 1024 - (AS if rnd else 0)
+        gather_d(rnd, 0, OP, "oP", 0, a0)
         if rnd == 0:
-            spread(0, 3)
-            spread(1, 4)
-        distance(0, OP, "oP", fine)
-        if rnd == 0:
-            spread_out(0, 3)
-        turn(0, "mD", T.SQ, 0, "SQ0")
-        space(0, 0)
-        if rnd == 0:
-            spread_out(1, 4)
-            mask(0)
-            neighbours()
-            low_offsets()
-            tt(sm("pid"), PT, sm("idc"), ALU.subtract, ["Lp", "idc"], ["pid"])
-        distance_out(0, 0, "mE", (0, 1, 2))
-        ts(T.off[:, OB:OB + 128], P[7][:, 0:128], 2048.0, ALU.add, ["P7"], ["oBA"])
-        tt(T.FL[:, 192:320], P[7][:, 0:128], T.L[:, 0:2, :], ALU.is_equal, ["P7", "Ln", "Lv"], ["f"])
-        distance(1, OA, "oBA", [(0, 512), (512, 1024)])
-        act(sm("e0"), P[0][:, 0:64], ["P0"], ["e0"], func=ACT.Copy)
-        turn(5, "mD", T.SQ, 1024, "SQ1")
-        distance(2, OB, "oBA", fine)
-        space(1, 5, "v")
-        distance_out(1, 5, "mH", (0, 2, 4))
-        turn(1, "mD", T.SQ, 2048, "SQ2")
-        space(2, 1)
-        distance_out(2, 1, "mH", (0, 1, 3))
-        mask(1)
-        tt(sm("ap"), P[7][:, 64:128], PT, ALU.subtract, ["P7", "Lp"], ["ap"])
-        tt(sm("bid"), P[7][:, 0:64], sm("idc"), ALU.subtract, ["P7", "idc"], ["bid"])
-        tt(sm("c"), P[5][:, 0:64], sm("e0"), ALU.is_lt, ["P5", "e0"], ["c"])
-        tt(sm("m01"), P[5][:, 0:64], sm("e0"), ALU.min, ["P5", "e0"], ["m01"])
-        tt(sm("t"), sm("c"), sm("ap"), ALU.mult, ["c", "ap"], ["t"])
-        ts(sm("v"), sm("m01"), T.col[:, 0:1], ALU.is_lt, ["m01", "th"], ["v"])
-        tt(sm("dq"), sm("t"), sm("pid"), ALU.add, ["t", "pid"], ["dq"])
-        ts(sm("mt"), sm("m01"), T.col[:, 0:1], ALU.min, ["m01", "th"], ["mt"])
+            for i, w in ((4, 0.125), (5, 0.5), (3, -256.0), (2, 2.0)):
+                act(T.mI[:, i, :], EYE, ["mI"], ["mL"], scale=w)
+            n_gather(NV0)
+            cp(T.mT[:, 72:80], T.mD[:], ["mD"], ["mV"])
+            cp(T.mO[:, 15:143:16], T.mD[:], ["mD", "mO"], ["mO"])
+            ts(T.mD[:], T.mD[:], DS, ALU.mult, ["mD"], ["mD", "mE"])
+            ts(T.thT[:, 1, :], T.thT[:, 1, :], 0.0, ALU.is_equal, ["iT", "th"], ["iT"], T.col[:, 0:1], ALU.mult)
+            n_turn()
+            mm([(pc(1, 0, 64), [(T.one[:], T.thT[:, 1, :])])], ["one", "iT"], ["P1"])
+            act(TH, pc(1, 0, 64), ["P1"], ["thT"])
+        spread(0)
+        spread(1)
+        ts(T.FL[:], pc(3, 192, 320), 0.0, ALU.is_equal, ["P3"], ["FL"])
+        if a0 < 1024:
+            move("a", T.GD[:, a0:1024], X.indirect(off(OP, a0 // 16, 64)), XK[rnd] + ["oP"], ["GD"], XB)
+            mm([(pc(4, 0, AS), [(NEG, T.xo[:, a0:1024]), (EYE, T.GD[:, a0:1024])])], ["mI", "mK", "GD"] + XO, ["P4"])
+        square(0, 0, a0)
+        if a0 < 1024:
+            act(T.SQ[:, a0:1024], pc(4, 0, AS), ["P4"], ["SQ0_a"], func=ACT.Square)
+        sums(0, EIGHTH, (2, 3, 4), [0, "a"])
+        for a, b in [(0, 512), (512, 1024)]:
+            gather_d(rnd, 1, OA, "oBA", a, b)
+            square(1, a, b)
+        sums(1, HALF, (1, 3, 4), (0, 512))
+        act(sm("e0"), pc(0, 0, 64), ["P0"], ["e0"])
+        for a, b in CUT2:
+            gather_d(rnd, 2, OB, "oBA", a, b)
+            square(2, a, b)
+        sums(2, HALF, (0, 2, 4), [c[0] for c in CUT2])
+        low()
+        mask(1, "a")
+        move("a", off(OL), pc(0, 0, 64), ["P0"], ["oL"], 2048.0 + 256 * XB)
+        tt(sm("c"), pc(1, 0, 64), sm("e0"), ALU.is_lt, ["P1", "e0"], ["c"])
+        tt(sm("m01"), pc(1, 0, 64), sm("e0"), ALU.min, ["P1", "e0"], ["m01"])
+        tt(sm("t"), pc(3, 128, 64), sm("c"), ALU.mult, ["c", "P3"], ["t"])
+        tt(sm("v"), sm("m01"), TH, ALU.is_lt, ["m01", "thT"], ["v"])
+        tt(sm("dq"), pc(3, 448, 64), sm("t"), ALU.add, ["t", "P3"], ["dq"])
+        tt(sm("mt"), sm("m01"), TH, ALU.min, ["m01", "thT"], ["mt"])
         tt(sm("t2"), sm("v"), sm("dq"), ALU.mult, ["v", "dq"], ["t2"])
-        tt(sm("dbp"), sm("bid"), sm("dq"), ALU.subtract, ["bid", "dq"], ["dbp"])
-        tt(sm("dbq"), sm("bid"), sm("t2"), ALU.subtract, ["bid", "t2"], ["dbq"])
-        tt(sm("q01"), sm("t2"), sm("idc"), ALU.add, ["t2", "idc"], ["q01"])
-        tt(sm("u1"), P[1][:, 0:64], sm("mt"), ALU.is_lt, ["P1", "mt"], ["u1"])
+        tt(sm("q01"), sm("t2"), tf(SI), ALU.add, ["t2", "tI"], ["q01"])
+        tt(sm("u1"), pc(2, 0, 64), sm("mt"), ALU.is_lt, ["P2", "mt"], ["u1"])
+        tt(sm("dbq"), pc(3, 0, 64), sm("q01"), ALU.subtract, ["P3", "q01"], ["dbq"])
         tt(sm("u2"), sm("u1"), sm("dbq"), ALU.mult, ["u1", "dbq"], ["u2"])
-        tt(T.q16[:], sm("u2"), sm("q01"), ALU.add, ["u2", "q01"], ["q16"])
-        to_table([(T.q16[:], "q16", 2, "d_t%d" % (2 + 3 * rnd))])
-        act(T.own[:], T.xo[:], ["xo0", "xo1"], ["own"], scale=2.0, bias=4.0 - 4.0 * M0)
-        tt(sm("u3"), P[1][:, 0:64], sm("m01"), ALU.is_lt, ["P1", "m01"], ["u3"])
-        ts(off(OQ), T.q16[:], 2048.0, ALU.add, ["q16"], ["oQ"])
-        tt(sm("u4"), sm("u3"), sm("dbp"), ALU.mult, ["u3", "dbp"], ["u4"])
-        tt(T.GA[:], T.CH[:, 512:768].indirect(off(OL)), T.MK[:], ALU.mult, ["CH2", "oL", "MK"], ["GA"])
-        mm([pick(P[2][:, 0:64], T.mO, 0, T.GA)], ["mO", "GA"], ["P2"])
-        tt(sm("pid"), sm("u4"), sm("dq"), ALU.add, ["u4", "dq"], ["pid"])
-        tt(PT, sm("pid"), sm("idc"), ALU.add, ["pid", "idc"], ["Lp"])
-        ts(off(OU), P[2][:, 0:64], 2048.0, ALU.add, ["P2"], ["oU"])
+        tt(tf(SW), sm("u2"), sm("q01"), ALU.add, ["u2", "q01", "TT"], ["tW"])
+        pieces(SW, "tW", 5)
+        table("a", RW, 5, "d_t%d" % (2 + 3 * rnd))
+        mm([back(4, 0, SW)], ["mG", "tW"], ["P4"])
+        mask(0, "v")
+        move("a", off(OW), pc(4, 0, 64), ["P4"], ["oW"], 2048.0)
+        acc([(pc(0, 0, 256), NEG, tf(SN, 4)), (pc(0, 192, 64), NEG, tf(SV))], ["mK", "tNV", "tI", "TT"], 0, True)
+        tt(T.GU[:], T.CH[:, 512:768].indirect(off(OL)), T.MK[:], ALU.mult, ["CH2", "oL", "MK0", "MK1"], ["GU"])
+        mm([(pc(7, 0, 64), [(T.mO[:, 15 - r:143 - r], T.GU[:, r:1024:16]) for r in range(16)])], ["mO", "GU"], ["P7"])
+        acc(turn(0, 64, 8, T.mT[:, 72:80], T.GU), ["mV", "GU"], 0)
+        tt(sm("p01"), sm("t"), tf(SP), ALU.add, ["t", "tP"], ["p01"])
+        tt(sm("u3"), pc(2, 0, 64), sm("m01"), ALU.is_lt, ["P2", "m01"], ["u3"])
+        tt(sm("dbp"), pc(3, 0, 64), sm("p01"), ALU.subtract, ["P3", "p01"], ["dbp"])
+        cols = [256 * d for d in (peers + [rank] if last else range(4))]
+        for i in range(2):
+            acc([(pc(SBANK[i], 0, 256), TWO, T.xo[:, cols[i]:cols[i] + 256])], ["mL"] + XO, SBANK[i], True)
+        ts(off(OU), pc(7, 0, 64), 2048.0, ALU.add, ["P7"], ["oU"])
+        act(T.GF[:], T.TB[:, 0:4096].indirect(off(OW)), TK + ["oW"], ["GF"])
         cp(T.GB[:], T.TB[:, 0:4096].indirect(off(OU)), TK + ["oU"], ["GB"])
-        act(T.GF[:], T.TB[:, 0:4096].indirect(off(OQ)), TK + ["oQ"], ["GF"], func=ACT.Copy)
-        mm([pick(P[4][:, 0:64], T.mZ, 288, T.GB)], ["mZ2", "GB"], ["P4"])
-        turn(3, "mK", T.GF, 0, "GF")
-        space(3, 3)
-        mm([(P[3][:, 0:64], turn_back(3, [(T.mQ[:], sm("idc"))])),
-            (P[3][:, 64:128], turn_back(3, [(T.mQ[:], sm("idc")), (T.mN[:], NX)]))], ["mG", "mQ", "mN", "idc", "Ln", "ZB3"], ["P3"])
-        act(sm("ab"), P[3][:, 0:64], ["P3"], ["ab"], func=ACT.Abs, bias=0.5)
-        act(T.cn[:], sm("ab"), ["ab"], ["cn"], func=ACT.Sigmoid, scale=-1000.0, bias=2048000.0)
-        tt(sm("du"), P[2][:, 0:64], PV, ALU.subtract, ["P2", "Lv"], ["du"])
+        tt(sm("u4"), sm("u3"), sm("dbp"), ALU.mult, ["u3", "dbp"], ["u4"])
+        tt(tf(SP), sm("u4"), sm("p01"), ALU.add, ["u4", "p01"], ["tP"])
+        acc(turn(0, 0, 24, T.mT[:, 40:64], T.GF), ["mT", "GF"], 0)
+        acc(turn(0, 192, 8, T.mT[:, 64:72], T.GB), ["mT", "GB"], 0, False, True)
         if not last:
-            ts(off(OP), PT, 2048.0, ALU.add, ["Lp"], ["oP"])
-        tt(sm("u2"), P[4][:, 0:64], PV, ALU.is_equal, ["P4", "Lv"], ["u2"])
-        tt(sm("u3"), sm("u2"), sm("du"), ALU.mult, ["u2", "du"], ["u3"])
-        tt(PV, sm("u3"), PV, ALU.add, ["u3", "Lv"], ["Lv"])
-        ts(off(OV), PV, 2048.0, ALU.add, ["Lv"], ["oV"])
-        if not last:
-            spread(0, 0)
-            spread(1, 1)
-            spread_out(0, 0)
-        tt(T.t1[:], T.X[:, 0:4096].indirect(off(OV)), T.own[:], ALU.add, XK + ["oV", "own"], ["t1"])
-        tt(sm("u4"), P[3][:, 64:128], T.cn[:], ALU.mult, ["P3", "cn"], ["u4"])
-        tt(NX, sm("u4"), NX, ALU.add, ["u4", "Ln"], ["Ln"])
-        ts(off(ON), NX, 2048.0, ALU.add, ["Ln"], ["oN"])
-        if not last:
-            to_table([(NX, "Ln", 0, "d_t%d" % (3 + 3 * rnd)), (PV, "Lv", 1, "d_t%d" % (4 + 3 * rnd))])
-            spread_out(1, 1)
-        else:
-            for n, d in enumerate(peers + [rank]):
-                mm([(P[4 + n][:, 256 + t:304:3],
-                     [(T.mF[:, 192 * d + 3 - j:192 * d + 131 - j], T.L[:, t, 16 * j:16 * j + 16]) for j in range(4)]
-                     + [(T.mI[:], T.c15[:])]) for t in range(3)], ["mF", "mI", "c15", "Ln", "Lv", "Lp"], ["P%d" % (4 + n)])
-        for h in range(2):
-            tt(T.S[:, 512 * h:512 * h + 512], T.X[:, 0:4096].indirect(off(ON, 32 * h, 32 * h + 32)), T.t1[:, 512 * h:512 * h + 512],
-               ALU.add, XK + ["oN", "t1"], ["S%d" % h])
-            if not last:
-                mm([(P[h][:], [(T.mI[:], T.S[:, 512 * h:512 * h + 512])])], ["mI", "S%d" % h], ["P%d" % h])
-                act(T.xo[:, 512 * h:512 * h + 512], P[h][:], ["P%d" % h], ["xo%d" % h], scale=WQ, bias=BQ)
-        if not last:
-            low_offsets()
-            for b in range(8):
-                k = (2 + b) % 6
-                mm([(P[k][:, 64 * r:64 * r + 64], [(T.mB[:, 128 * (b // 2):128 * (b // 2) + 128], T.S[:, 8 * (b % 2) + r:1024:16])])
-                    for r in range(8)], ["mB", "S0", "S1"], ["P%d" % k])
-                o = T.X[:, 512 * b:512 * b + 512]
-                if b in (0, 2, 4):
-                    ts(o, P[k][:], WQ, ALU.mult, ["P%d" % k], [XK[b]], BQ, ALU.add)
-                else:
-                    act(o, P[k][:], ["P%d" % k], [XK[b]], scale=WQ, bias=BQ)
-            flags()
-            mask(0)
-            neighbours()
+            mm([back(6, 0, SP)], ["mG", "tP"], ["P6"])
+            move("a", off(OP), pc(6, 0, 64), ["P6"], ["oP"], 2048.0)
+        ts(sm("cc", 2), pc(0, 128, 128), 0.0, ALU.is_equal, ["P0"], ["cc"])
+        tt(sm("ee", 2), pc(0, 0, 128), sm("cc", 2), ALU.mult, ["P0", "cc"], ["ee"])
+        tt(tf(SN, 2), sm("ee", 2), tf(SN, 2), ALU.add, ["ee", "tNV"], ["tNV"])
+        mm([back(4, 0, SV)], ["mG", "tNV"], ["P4"])
+        mm([back(5, 0, SN), back(5, 64, SV)], ["mG", "tNV"], ["P5"])
+        ts(off(OV), pc(4, 0, 64), 2048.0, ALU.add, ["P4"], ["oV"])
+        move("a", off(ON), pc(5, 0, 64), ["P5"], ["oN"], 2048.0)
 
-    for n, d in enumerate(peers + [rank]):
-        k = 4 + n
-        mm([(P[k][:, 64 * r:64 * r + 64],
-             [(T.mW[:, 192 * d + 3 - j:192 * d + 131 - j], T.S[:, 4 * j + r:1024:16]) for j in range(4)]) for r in range(4)],
-           ["mW", "S0", "S1"], ["P%d" % k])
-        buf, key = (T.lx, "lx%d" % d) if d == rank else (T.sx, "sx%d" % d)
-        ts(buf[:, d, :], P[k][:, 0:304], BQ, ALU.add, ["P%d" % k], [key], M0, ALU.subtract)
-        if d != rank:
-            send(1, d, T.lx[:, rank, :], T.sx[:, d, :], key)
-            arrives(1, d, "lx%d" % d)
-    for n, d in enumerate([rank] + peers):
-        if n == 3:
-            for s in range(2):
-                ts(T.lf[:, :, s, :], T.lx[:, :, 256:304], T.col[:, 4 + s:5 + s], ALU.mult, ["ms"] + ["lx%d" % i for i in range(4)], ["lf"])
-        cp(T.ox[:, d, :], T.lx[:, d, 0:256], ["lx%d" % d], ["ox%d" % d])
+        def gathers(i):
+            a, k = cols[i], SBANK[i]
+            cp(T.G1[:, a:a + 256], X.indirect(off(OV, a // 16, a // 16 + 16)), XK[rnd] + ["oV"], ["G1_%d" % i])
+            act(T.G2[:, a:a + 256], X.indirect(off(ON, a // 16, a // 16 + 16)), XK[rnd] + ["oN"], ["G2_%d" % i])
+
+        def add_up(i):
+            a, k = cols[i], SBANK[i]
+            acc(([(pc(k, 0, 256), TWO, T.xo[:, a:a + 256])] if i > 1 else [])
+                + [(pc(k, 0, 256), EYE, T.G1[:, a:a + 256]), (pc(k, 0, 256), EYE, T.G2[:, a:a + 256])],
+                ["mI", "mL", "G1_%d" % i, "G2_%d" % i, XO[a // 256]], k, i > 1, True)
+
+        def mean(i, e):
+            a, k = cols[i], SBANK[i]
+            if e == "v":
+                ts(T.xo[:, a:a + 256], pc(k, 0, 256), 0.25, ALU.mult, ["P%d" % k], [XO[a // 256]], XB / 2 - 0.375, ALU.add)
+            else:
+                act(T.xo[:, a:a + 256], pc(k, 0, 256), ["P%d" % k], [XO[a // 256]], func=ACT.Identity, scale=0.25, bias=XB / 2 - 0.375)
+
+        if not last:
+            for step in SMOOTH.split():
+                w, e, i = step[0].lower(), "v" if step[0].isupper() else "a", int(step[1:] or 0)
+                if w == "g":
+                    gathers(i)
+                elif w == "s":
+                    add_up(i)
+                elif w == "p":
+                    pieces((SV, SN)[i], "tNV", 6 + i)
+                elif w == "f":
+                    flags_sum()
+                elif w == "c":
+                    table(e, (RV, RN)[i], 6 + i, "d_t%d" % (3 + i + 3 * rnd))
+                elif w == "x":
+                    mean(i, e)
+                elif w == "h":
+                    high(5, 64)
+                elif w == "b":
+                    k = BBANK[i]
+                    mm([(P[k][:, :, q, :], [(T.mB[:, 128 * q:128 * q + 128], T.xo[:, 128 * i:128 * i + 128])]) for q in range(4)],
+                       ["mB", XO[i // 2]], ["P%d" % k])
+                    move(e, XT[rnd + 1][:, 512 * i:512 * i + 512], pc(k, 0, 512), ["P%d" % k], [XK[rnd + 1][i]], -XB)
+                elif w == "n":
+                    n_gather(0)
+                else:
+                    n_turn()
+
+    def home(n):
+        d, k = (peers + [rank])[n], 4 + n
+        mm([(P[k][:, 0:8, q, :], [(T.mF[:, 192 * q + 3 - j:192 * q + 131 - j], T.xo[:, 256 * d + 64 * j:256 * d + 64 * j + 64]) for j in range(4)])
+            for q in range(4)], ["mF", XO[d]], ["P%d" % k])
+
+    def leave(n, e):
+        d, k = (peers + [rank])[n], 4 + n
+        if d == rank:
+            move(e, T.ox[:, d, :], pc(k, 0, 256), ["P%d" % k], ["ox%d" % d], -XB)
+            dmas("s", "d_out", [(T.yx[32 * d:32 * d + 32, :], T.ox[:, d, :])], ["ox%d" % d], [])
+        else:
+            move(e, T.sx[:, d, 0:256], pc(k, 0, 256), ["P%d" % k], ["sx%d" % d])
+            w = 256 if n == 2 else 304
+            send(3, d, T.lx[:, rank, 0:w], T.sx[:, d, 0:w], ["sy", "sx%d" % d], "lx%d" % d)
+
+    gathers(0)
+    LB = (3, 6, 7, 0)
+    for d in range(4):
+        mm([(P[LB[d]][:, t, 0:2, :],
+             [(T.mZ[32 * d:32 * d + 32, 65 + 64 * d - 64 * s - j:193 + 64 * d - 64 * s - j],
+               T.TT[32 * d:32 * d + 32, 16 * slot + 1 + 8 * s + 4 * j:16 * slot + 5 + 8 * s + 4 * j:2, :]) for s in range(2) for j in range(2)])
+            for t, slot in enumerate((SN, SV, SP))], ["mZ", "tNV", "tP"], ["P%d" % LB[d]])
+    add_up(0)
+    gathers(1)
+    for d in range(4):
+        move("a", T.sx[:, d, 256:304], P[LB[d]][:, 0:3, 0:2, :], ["P%d" % LB[d]], ["sy"])
+    mean(0, "v")
+    add_up(1)
+    home(0)
+    send(2, peers[2], T.lx[:, rank, 256:304], T.sx[:, peers[2], 256:304], ["sy"], "ly%d" % peers[2])
+    gathers(2)
+    leave(0, "v")
+    mean(1, "a")
+    add_up(2)
+    home(1)
+    gathers(3)
+    leave(1, "a")
+    mean(2, "v")
+    add_up(3)
+    home(2)
+    leave(2, "v")
+    mean(3, "a")
+    home(3)
+    leave(3, "a")
+    ts(T.col[:, 4:5], T.pi[:, 0:1], 64.0, ALU.is_lt, ["pi0"], ["ms"])
+    ts(T.col[:, 5:6], T.pi[:, 0:1], 64.0, ALU.is_ge, ["pi0"], ["ms"])
+
+    def halves(d, src, key):
+        for s in range(2):
+            ts(T.lf[:, :, d, s, :], src[:, d, 256:304], T.col[:, 4 + s:5 + s], ALU.mult, ["ms", key], ["lf"])
+
+    halves(rank, T.sx, "sy")
+    halves(peers[2], T.lx, "ly%d" % peers[2])
+    for n, d in enumerate(peers):
+        move("av"[n // 2], T.ox[:, d, :], T.lx[:, d, 0:256], ["lx%d" % d], ["ox%d" % d], -XB)
         dmas("s", "d_out", [(T.yx[32 * d:32 * d + 32, :], T.ox[:, d, :])], ["ox%d" % d], [])
-    mm([(P[0][:, 64 * t:64 * t + 64], [(T.lf[:, :, :, t:48:3], T.mJ[:])]) for t in range(3)], ["mJ", "lf"], ["P0"])
-    act(T.yl[:], P[0][:, 0:192], ["P0"], ["yl"], bias=2048.0)
-    dmas("a", "d_out", [(T.yn[:], T.yl[:, 0:64]), (T.yv[:], T.yl[:, 64:128]), (T.yp[:], T.yl[:, 128:192])], ["yl"], [])
+        if n < 2:
+            halves(d, T.lx, "lx%d" % d)
+        if n == 1:
+            mm([(pc(0, 64 * t, 64), [(T.lf[:, t, :, :, :], T.mJ[:])]) for t in range(3)], ["mJ", "lf"], ["P0"])
+            move("a", T.yl[:], pc(0, 0, 192), ["P0"], ["yl"], 2048.0)
+            dmas("a", "d_out", [(T.yn[:], T.yl[:, 0:64]), (T.yv[:], T.yl[:, 64:128]), (T.yp[:], T.yl[:, 128:192])], ["yl"], [])
     for s, v in total.items():
         g.wait_ge(T.sem[s], v)

from concourse.mybir import AluOpType as ALU, ActivationFunctionType as ACT

F32, F16, BF, I32, U16 = "float32", "float16", "bfloat16", "int32", "uint16"
SCRATCH = {
    "xi": ("sbuf", [128, 4, 256], I32), "li": ("sbuf", [128, 192], I32), "thi": ("sbuf", [128, 4], I32),
    "zb": ("sbuf", [128, 1160], BF), "lz": ("sbuf", [128, 448], F16),
    "snd": ("sbuf", [128, 4, 304], F16), "lnd": ("sbuf", [128, 4, 304], F16),
    "iS": ("sbuf", [128, 64], BF), "iR": ("sbuf", [128, 128], BF), "iW": ("sbuf", [128, 128], BF), "iK": ("sbuf", [128, 64], F32),
    "mX": ("sbuf", [128, 2048], BF), "mO": ("sbuf", [128, 144], BF), "mI": ("sbuf", [128, 6, 128], BF),
    "mS": ("sbuf", [128, 128], BF), "mR": ("sbuf", [128, 512], BF), "mP": ("sbuf", [128, 128], BF),
    "mW": ("sbuf", [128, 1088], BF), "mF": ("sbuf", [128, 768], BF), "mZ": ("sbuf", [128, 400], BF), "mB": ("sbuf", [128, 512], BF),
    "mT": ("sbuf", [128, 80], BF), "mD": ("sbuf", [128, 8], F32), "mG": ("sbuf", [128, 128], BF),
    "mJ": ("sbuf", [128, 64], BF), "col": ("sbuf", [128, 16], F32), "one": ("sbuf", [128, 128], F32),
    "pi": ("sbuf", [128, 16], I32), "thT": ("sbuf", [128, 2, 64], F32),
    "TT": ("sbuf", [128, 145, 8], F16), "FL": ("sbuf", [128, 320], BF), "MK": ("sbuf", [128, 1024], BF),
    "X0": ("sbuf", [128, 4096], BF), "X1": ("sbuf", [128, 4096], BF), "TB": ("sbuf", [128, 4096], F32),
    "xo": ("sbuf", [128, 1024], F16), "D": ("sbuf", [128, 3072], F16), "SQ": ("sbuf", [128, 3072], F32),
    "GN": ("sbuf", [128, 1024], F16), "GU": ("sbuf", [128, 1024], F16), "GB": ("sbuf", [128, 1024], F16),
    "GF": ("sbuf", [128, 1024], F16), "G1": ("sbuf", [128, 1024], F16), "G2": ("sbuf", [128, 1024], F16),
    "GD": ("sbuf", [128, 1024], F16), "AB": ("sbuf", [128, 512], F32), "hi": ("sbuf", [128, 64], F16),
    "CH": ("sbuf", [128, 768], F32), "off": ("sbuf", [128, 576], U16), "sm": ("sbuf", [128, 64 * 24], F32),
    "lf": ("sbuf", [128, 3, 4, 2, 16], F16), "yl": ("sbuf", [128, 192], F32),
    "sx": ("sbuf", [128, 4, 304], F16), "lx": ("sbuf", [128, 4, 304], F16), "ox": ("sbuf", [128, 4, 256], F32),
}
for _b in range(8):
    SCRATCH["P%d" % _b] = ("psum", [128, 16, 4, 8], F32)
SEMAPHORES = (["c_v", "c_a", "c_pe", "c_g", "sent", "d_li", "d_th", "d_out"] + ["d_x%d" % i for i in range(4)]
              + ["d_t%d" % i for i in range(9)] + ["a%d_%d" % (i, j) for i in range(4) for j in range(4)])

XB = 1280.0
DS = 2.0 ** -23
RO = 3
SN, SV, SI, SZ, SP, SB, SA, SW = 0, 1, 2, 3, 5, 6, 7, 8
RV, RN, RW = 0, 1, 2
PARTS = ["lz", "mS", "T0", "T1", "T2", "sl", "sy", "mX", "mF", "mR", "mW", "mL", "mT", "ms", "lf", "mB"]
AS = 512
NV0 = 512
CUT2 = [(0, 512), (512, 768), (768, 1024)]
SMOOTH = "g0 p0 p1 s0 g1 s1 C0 c1 g2 X0 s2 g3 x1 h B0 s3 b1 X2 B2 x3 n f B3 B4 B5 B6 b7 t"
SBANK = (1, 2, 0, 1)
BBANK = (4, 6, 7, 2, 0, 4, 6, 7)


def rank_program(g, core, T, topo):
    rank = T.rank_of(core)
    if rank is None:
        return
    Q = {"v": g.vector, "a": g.scalar, "pe": g.tensor, "g": g, "s": g.sync}
    total, seen, state = {}, {}, {}

    def wait(e, tok):
        if seen.get((e, tok[0]), 0) < tok[1]:
            seen[(e, tok[0])] = tok[1]
            Q[e].wait_ge(T.sem[tok[0]], tok[1])

    def deps(e, reads, writes):
        for k in reads:
            st = state.setdefault(k, {"w": {}, "r": {}})
            for t in st["w"].values():
                wait(e, t)
            if k[0] == "P":
                for t in st["r"].values():
                    if t[2] != e:
                        wait(e, t)
        for k in writes:
            st = state.setdefault(k, {"w": {}, "r": {}})
            for t in list(st["w"].values()) + list(st["r"].values()):
                if t[2] != e or not (e == "pe" or (k in PARTS and not st["r"])):
                    wait(e, t)

    def mark(tok, reads, writes):
        for k in reads:
            state[k]["r"][tok[0]] = tok
        for k in writes:
            state[k] = {"w": {tok[0]: tok}, "r": {}}

    def op(e, fn, reads, writes):
        deps(e, reads, writes)
        s = "c_" + e
        total[s] = total.get(s, 0) + 1
        fn().then_inc(T.sem[s], 1)
        mark((s, total[s], e), reads, writes)

    def dmas(e, sem, pairs, reads, writes):
        deps(e, reads, writes)
        for o, i in pairs:
            total[sem] = total.get(sem, 0) + 16
            Q[e].dma_start(o, i).then_inc(T.sem[sem], 16)
        mark((sem, total[sem], "dma"), reads, writes)

    def mm(groups, reads, writes):
        def fn():
            last = None
            for out, terms in groups:
                for n, (a, b) in enumerate(terms):
                    last = g.tensor.matmul(out, a, b, n == 0, n == len(terms) - 1)
            return last
        op("pe", fn, reads, writes)

    def acc(terms, reads, bank, start=False, stop=False):
        def fn():
            last = None
            for n, (out, a, b) in enumerate(terms):
                last = g.tensor.matmul(out, a, b, start and n == 0, stop and n == len(terms) - 1)
            return last
        op("pe", fn, reads, ["P%d" % bank])

    def tt(o, a, b, alu, reads, writes):
        op("v", lambda: g.vector.tensor_tensor(o, a, b, alu), reads, writes)

    def ts(o, a, s1, op0, reads, writes, s2=None, op1=None):
        if op1 is None:
            op("v", lambda: g.vector.tensor_scalar(o, a, s1, None, op0), reads, writes)
        else:
            op("v", lambda: g.vector.tensor_scalar(o, a, s1, s2, op0, op1), reads, writes)

    def cp(o, a, reads, writes):
        op("v", lambda: g.vector.tensor_copy(o, a), reads, writes)

    def fill(o, c, keys):
        op("v", lambda: g.vector.memset(o, c), [], keys)

    def act(o, a, reads, writes, func=ACT.Copy, **kw):
        op("a", lambda: g.scalar.activation(o, a, func, **kw), reads, writes)

    def move(e, o, a, reads, writes, add=None):
        if add is None:
            (cp if e == "v" else act)(o, a, reads, writes)
        elif e == "v":
            ts(o, a, add, ALU.add, reads, writes)
        else:
            act(o, a, reads, writes, func=ACT.Identity, bias=add)

    def iota(o, pat, base, cm, key):
        op("g", lambda: g.iota(o, pat, base, cm, allow_small_or_imprecise_dtypes=True), [], [key])

    def dots(o, src, skey, pat, base, val, key, alu=ALU.not_equal, cm=-1):
        op("g", lambda: g.affine_select(o, src, pat, alu, val, base, cm), [skey], [key])

    def send(phase, d, dst, src, keys, land):
        deps("g", keys, [])
        rid, pid = topo.addr(T.cores[d])[:2]
        total["sent"] = total.get("sent", 0) + len(topo.engines(core, T.cores[d]))
        g.remote_dma(dst, src, T.sem["a%d_%d" % (phase, rank)], T.sem["sent"], pid, rid, topo.mask(core, T.cores[d]))
        s = "a%d_%d" % (phase, d)
        total[s] = len(topo.engines(T.cores[d], core))
        state[land] = {"w": {s: (s, total[s], "rem")}, "r": {}}

    def far(d):
        a, b = topo.chip(core), topo.chip(T.cores[d])
        return 2 if topo.mates(a, b) else 1 if topo.same_plane(a, b) else 0
    peers = sorted([d for d in range(4) if d != rank], key=far)

    slots = {}

    def sm(name, n=1):
        if name not in slots:
            slots[name] = len(slots)
            for i in range(1, n):
                slots[name + str(i)] = len(slots)
        return T.sm[:, 64 * slots[name]:64 * (slots[name] + n)]

    OP, OB, OA, ON, OV, OW, OU, OI, OL = [64 * i for i in range(9)]

    def off(c, a=0, b=64):
        return T.off[:, c + a:c + b]

    def tf(a, n=1):
        return T.TT[:, 16 * a + 1:16 * (a + n):2, :]

    P = [T["P%d" % b] for b in range(8)]

    def pc(b, a, n):
        return P[b][:, a // 32:(a + n) // 32, :, :]

    TK = ["T0", "T1", "T2"]
    XO = ["xo0", "xo1", "xo2", "xo3"]
    XT = [T.X0, T.X1, T.X0]
    XK = [["X%d_%d" % (r % 2, b) for b in range(8)] for r in range(RO)]
    EYE, NEG, TWO, M256, EIGHTH, HALF = [T.mI[:, i, :] for i in range(6)]
    TH = T.thT[:, 0, :]

    for n, d in enumerate(peers + [rank]):
        dmas("s", "d_x%d" % d, [(T.xi[:, d, :], T.x[32 * d:32 * d + 32, :])], [], ["xi%d" % d])
        if n == 0:
            dmas("a", "d_li", [(T.li[:, 0:64], T.nxt[:]), (T.li[:, 64:128], T.prv[:])], [], [])
            dmas("s", "d_li", [(T.li[:, 128:192], T.ptn[:])], [], ["li"])
    dmas("s", "d_th", [(T.thi[:, 0:1], T.th[:])], [], ["thi"])

    iota(T.iS[:], [[32, 4], [1, 16]], 0, -1, "iS")
    iota(T.iR[:], [[64, 2], [0, 4], [4, 16]], 0, -1, "iR")
    iota(T.iW[:], [[1000, 2], [0, 4], [8, 16]], 0, -1, "iW")
    op("g", lambda: g.iota(T.pi[:, 0:1], [[1, 1]], 0, 1), [], ["pi0"])
    iota(T.iK[:], [[0, 2], [1, 32]], -2048, 32, "iK")
    fill(T.zb[:, 0:512], 0.0, ["zb"])
    cp(T.lz[:], T.zb[:, 0:448], ["zb"], ["lz0"])
    for h in range(2):
        ts(T.mS[:, 64 * h:64 * h + 64], T.iS[:], -16.0 * h, ALU.is_equal, ["iS"], ["mS"])
    fill(T.zb[:, 512:1160], 0.0, ["zc"])
    dots(T.mP[:], T.zb[:, 0:128], "zb", [[64, 2], [1, 2], [2, 32]], 0, 1.0, "mP")
    for j in range(4):
        ts(T.mR[:, 128 * j:128 * j + 128], T.iR[:], -1.0 * j, ALU.is_equal, ["iR"], ["mR"])
    for b in range(8):
        act(T.TB[:, 512 * b:512 * b + 512], T.zb[:, 0:512], ["zb"], TK)

    for n, d in enumerate(peers + [rank]):
        key = ("lnd%d" if d == rank else "snd%d") % d
        ts(T.snd[:, d, 0:256], T.xi[:, d, :], XB, ALU.add, ["xi%d" % d], [key])
        if n == 0:
            send(1, d, T.lnd[:, rank, 0:256], T.snd[:, d, 0:256], [key], "lnd%d" % d)
            for t in range(3):
                ts(T.lz[:, 64 + 128 * t:128 + 128 * t], T.li[:, 64 * t:64 * t + 64], -2048.0, ALU.add, ["li", "lz0"], ["lz"])
            mm([(pc(0, 64 * t, 64), [(T.lz[:, 128 * t + 64 - 64 * h:128 * t + 192 - 64 * h], T.mS[:, 64 * h:64 * h + 64]) for h in range(2)])
                for t in range(3)], ["lz", "mS"], ["P0"])
            for t in range(3):
                cp(T.snd[:, :, 256 + 16 * t:272 + 16 * t], pc(0, 64 * t, 64), ["P0"], ["sl"])
        elif n < 3:
            send(1, d, T.lnd[:, rank, :], T.snd[:, d, :], [key, "sl"], "lnd%d" % d)
        if n == 2:
            send(0, peers[0], T.lnd[:, rank, 256:304], T.snd[:, peers[0], 256:304], ["sl"], "ll%d" % peers[0])

    def landed(q):
        return T.snd if q == rank else T.lnd

    cp(T.mW[:, 0:64], T.zb[:, 0:64], ["zb"], ["mW"])
    for j in range(8):
        ts(T.mW[:, 64 + 128 * j:192 + 128 * j], T.iW[:], -1.0 * j, ALU.is_equal, ["iW"], ["mW"])
    cp(T.TT[:], T.zb[:], ["zb", "zc"], ["TT"])
    dots(T.mG[:], T.zb[:, 0:128], "zb", [[1, 2], [2, 64]], 0, 1.0, "mG")
    dots(EYE, T.zb[:, 0:128], "zb", [[1, 128]], 0, 1.0, "mI")
    dots(NEG, T.zb[:, 0:128], "zb", [[1, 128]], 0, -1.0, "mK")
    for c, pat, row in ((0, [[1, 2]], RV), (16, [[0, 1]], RN), (24, [[1, 2]], RV), (40, [[1000, 2]], RN), (56, [[0, 2]], RW)):
        dots(T.mT[:, c:c + 8 * pat[0][1]], T.zb[:, 0:8 * pat[0][1]], "zb", pat + [[16, 8]], row, 1.0, "mT")
    iota(T.mD[:], [[0, 8]], 1, 0, "mD")
    dots(T.mD[:], T.mD[:], "mD", [[16, 8]], 15, 0.0, "mD", ALU.is_ge)
    dots(T.mD[:], T.mD[:], "mD", [[-16, 8]], 0, 0.0, "mD", ALU.is_ge, 1)
    iota(T.thT[:, 1, :], [[16, 2], [0, 32]], 32 * rank, -1, "iT")
    iota(T.one[:], [[0, 128]], 1, 0, "one")
    for j in range(4):
        dots(T.mX[:, 512 * j:512 * j + 512], T.zb[:, 0:512], "zb", [[1, 4], [16, 8], [0, 16]], 4 * j, 1.0, "mX")
    for j in range(4):
        dots(T.mB[:, 128 * j:128 * j + 128], T.zb[:, 0:128], "zb", [[64, 2], [0, 4], [1, 16]], 16 * j, 1.0, "mB")
    for j in range(4):
        dots(T.mF[:, 192 * j:192 * j + 192], T.zb[:, 0:192], "zb", [[64, 3], [1, 16], [1000, 4]], 16 * j - 3000, 1.0, "mF")
    dots(T.mZ[:], T.zb[:, 0:400], "zb", [[1, 400]], -65, 1.0, "mZ", cm=-2)
    dots(T.mJ[:], T.zb[:, 0:64], "zb", [[1, 64]], 0, 1.0, "mJ")
    dots(T.mJ[:], T.mJ[:], "mJ", [[1, 64]], 64, 1.0, "mJ")
    ts(T.pi[:, 4:5], T.pi[:, 0:1], 15, ALU.bitwise_and, ["pi0"], ["pi1"])
    act(tf(SI), T.iK[:], ["iK", "TT"], ["tI"])
    move("a", T.col[:, 6:7], T.pi[:, 4:5], ["pi1"], ["rc"], XB)

    def pieces(slot, key, bank):
        mm([(P[bank][:, j, :, :], [(T.mW[:, 64 + 128 * j - 64 * s:192 + 128 * j - 64 * s], T.TT[:, 16 * slot + 1 + 8 * s:16 * slot + 9 + 8 * s:2, :])
                                   for s in range(2)]) for j in range(8)], ["mW", key], ["P%d" % bank])

    def table(e, row, bank, sem):
        move(e, T.CH[:, 256 * row:256 * row + 256], pc(bank, 0, 256), ["P%d" % bank], ["CH%d" % row])
        dmas("s", sem, [(T.TB[row::16, :], T.CH[:, 256 * row:256 * row + 256])], ["CH%d" % row], [TK[row]])

    def turn(bank, col, n, w, src):
        return [(P[bank][:, col // 32:(col + 8 * n) // 32, :, r], src[:, r:1024:8], w) for r in range(8)]

    def back(bank, col, slot):
        return (pc(bank, col, 64), [(T.TT[:, 16 * slot + 1 - h:16 * slot + 17 - h, :], T.mG[:, 64 * h:64 * h + 64]) for h in range(2)])

    def high(bank, col):
        act(T.hi[:], pc(bank, col, 64), ["P%d" % bank], ["hi"], func=ACT.Identity, scale=1.0 / 256, bias=XB + 8.0 - 127.5 / 256)

    def low():
        o, terms = back(0, 0, SV)
        mm([(o, terms + [(M256, T.hi[:])])], ["mG", "mL", "tNV", "hi"], ["P0"])

    def flags_sum():
        acc([(pc(3, 0, 512), EYE, T.zb[:, 0:512]), (pc(3, 128, 64), NEG, tf(SP)), (pc(3, 192, 128), NEG, tf(SN, 2)), (pc(3, 320, 192), NEG, tf(SN, 3))]
            + [(pc(3, 320 + 64 * n, 64), EYE, tf(SP)) for n in range(3)], ["mI", "mK", "tNV", "tI", "tP", "zb"], 3, True)

    def n_gather(nv):
        act(T.GN[:, nv:1024], T.TB[:, 0:4096].indirect(off(OP, nv // 16, 64)), TK + ["oP"], ["GN1"])
        if nv:
            cp(T.GN[:, 0:nv], T.TB[:, 0:4096].indirect(off(OP, 0, nv // 16)), TK + ["oP"], ["GN0"])

    def n_turn():
        acc(turn(3, 0, 40, T.mT[:, 0:40], T.GN), ["mT", "GN0", "GN1"], 3, False, True)
        act(tf(SB, 2), pc(3, 0, 128), ["P3", "TT"], ["tBA"])
        mm([back(5, 0, SB), back(5, 64, SA)], ["mG", "tBA"], ["P5"])
        move("a", T.off[:, OB:OB + 128], pc(5, 0, 128), ["P5"], ["oBA"], 2048.0)

    def first_block(n, q):
        for hb in range(2):
            b = 4 + (2 * n + hb) % 4
            mm([(pc(b, 256 * jj, 256), [(T.mR[:, 128 * (2 * hb + jj):128 * (2 * hb + jj) + 128], landed(q)[:, q, 0:256])]) for jj in range(2)],
               ["mR", "lnd%d" % q], ["P%d" % b])
            move("va"[hb], T.X0[:, 1024 * q + 512 * hb:1024 * q + 512 * hb + 512], pc(b, 0, 512), ["P%d" % b], [XK[0][2 * q + hb]], -XB)

    def first_lists(q, key):
        mm([(P[2][32 * q:32 * q + 32, s:6:2, 2 * j:2 * j + 2, :], [(T.mP[:, 64 * s + 32 * j:64 * s + 32 * j + 32], landed(q)[:, q, 256:304])])
            for s in range(2) for j in range(2)], ["mP", key], ["P2"])

    def gather_d(rnd, n, oc, okey, a, b):
        tt(T.D[:, 1024 * n + a:1024 * n + b], XT[rnd][:, 0:4096].indirect(off(oc, a // 16, b // 16)), T.xo[:, a:b], ALU.subtract,
           XK[rnd] + [okey] + XO, ["D%d_%d" % (n, a)])

    def square(n, a, b):
        act(T.SQ[:, 1024 * n + a:1024 * n + b], T.D[:, 1024 * n + a:1024 * n + b], ["D%d_%d" % (n, a)], ["SQ%d_%d" % (n, a)],
            func=ACT.Square, bias=XB)

    def sums(n, m, fl, keys):
        acc([(pc(n, 0, 64), m, T.FL[:, 64 * f:64 * f + 64]) for f in fl], ["mL", "FL"], n, True)
        acc([(P[n][:, 0:2, :, r], T.SQ[:, 1024 * n + r:1024 * n + 1024:8], T.mD[:]) for r in range(8)],
            ["mE"] + ["SQ%d_%s" % (n, k) for k in keys], n, False, True)

    def spread(h):
        mm([(P[6 + h][:, :, r // 8::2, r % 8], [(T.mX[:, 128 * r:128 * r + 128], T.hi[:, 32 * h:32 * h + 32])]) for r in range(16)],
           ["mX", "hi"], ["P%d" % (6 + h)])

    def mask(h, e):
        o = T.MK[:, 512 * h:512 * h + 512]
        if e == "v":
            ts(o, pc(6 + h, 0, 512), T.col[:, 6:7], ALU.is_equal, ["P%d" % (6 + h), "rc"], ["MK%d" % h])
        else:
            act(T.AB[:], pc(6 + h, 0, 512), ["P%d" % (6 + h), "rc"], ["AB"], func=ACT.Abs, bias=T.col[:, 6:7], scale=-1.0)
            act(o, T.AB[:], ["AB"], ["MK%d" % h], func=ACT.Relu, scale=-1.0, bias=1.0)

    first_block(0, rank)
    first_block(1, peers[0])
    cp(T.mO[:], T.zb[:, 0:144], ["zb"], ["mO"])
    ts(T.col[:, 0:1], T.thi[:, 0:1], DS, ALU.mult, ["thi"], ["th"])
    first_lists(rank, "sl")
    first_block(2, peers[1])
    first_lists(peers[1], "lnd%d" % peers[1])
    mm([back(1, 0, SI)], ["mG", "tI"], ["P1"])
    move("a", off(OI), pc(1, 0, 64), ["P1"], ["oI"], 2048.0)
    first_block(3, peers[2])
    first_lists(peers[2], "lnd%d" % peers[2])
    first_lists(peers[0], "ll%d" % peers[0])
    cp(tf(SN, 2), pc(2, 0, 128), ["P2", "TT"], ["tNV"])
    pieces(SV, "tNV", 1)
    pieces(SN, "tNV", 0)
    act(tf(SP), pc(2, 128, 64), ["P2", "TT"], ["tP"])
    table("v", RV, 1, "d_t0")
    table("a", RN, 0, "d_t1")
    mm([back(4, 0, SP), back(4, 64, SV)], ["mG", "tP", "tNV"], ["P4"])
    for h in range(2):
        move("va"[h], T.xo[:, 512 * h:512 * h + 512], T.X0[:, 0:4096].indirect(off(OI, 32 * h, 32 * h + 32)), XK[0] + ["oI"], XO[2 * h:2 * h + 2], XB)
    ts(off(OP), pc(4, 0, 64), 2048.0, ALU.add, ["P4"], ["oP"])
    high(4, 64)
    flags_sum()

    for rnd in range(RO):
        last = rnd == RO - 1
        X = XT[rnd][:, 0:4096]
        a0 = 1024 - (AS if rnd else 0)
        gather_d(rnd, 0, OP, "oP", 0, a0)
        if rnd == 0:
            for i, w in ((4, 0.125), (5, 0.5), (3, -256.0), (2, 2.0)):
                act(T.mI[:, i, :], EYE, ["mI"], ["mL"], scale=w)
            n_gather(NV0)
            cp(T.mT[:, 72:80], T.mD[:], ["mD"], ["mV"])
            cp(T.mO[:, 15:143:16], T.mD[:], ["mD", "mO"], ["mO"])
            ts(T.mD[:], T.mD[:], DS, ALU.mult, ["mD"], ["mD", "mE"])
            ts(T.thT[:, 1, :], T.thT[:, 1, :], 0.0, ALU.is_equal, ["iT", "th"], ["iT"], T.col[:, 0:1], ALU.mult)
            n_turn()
            mm([(pc(1, 0, 64), [(T.one[:], T.thT[:, 1, :])])], ["one", "iT"], ["P1"])
            act(TH, pc(1, 0, 64), ["P1"], ["thT"])
        spread(0)
        spread(1)
        ts(T.FL[:], pc(3, 192, 320), 0.0, ALU.is_equal, ["P3"], ["FL"])
        if a0 < 1024:
            move("a", T.GD[:, a0:1024], X.indirect(off(OP, a0 // 16, 64)), XK[rnd] + ["oP"], ["GD"], XB)
            mm([(pc(4, 0, AS), [(NEG, T.xo[:, a0:1024]), (EYE, T.GD[:, a0:1024])])], ["mI", "mK", "GD"] + XO, ["P4"])
        square(0, 0, a0)
        if a0 < 1024:
            act(T.SQ[:, a0:1024], pc(4, 0, AS), ["P4"], ["SQ0_a"], func=ACT.Square)
        sums(0, EIGHTH, (2, 3, 4), [0, "a"])
        for a, b in [(0, 512), (512, 1024)]:
            gather_d(rnd, 1, OA, "oBA", a, b)
            square(1, a, b)
        sums(1, HALF, (1, 3, 4), (0, 512))
        act(sm("e0"), pc(0, 0, 64), ["P0"], ["e0"])
        for a, b in CUT2:
            gather_d(rnd, 2, OB, "oBA", a, b)
            square(2, a, b)
        sums(2, HALF, (0, 2, 4), [c[0] for c in CUT2])
        low()
        mask(1, "a")
        move("a", off(OL), pc(0, 0, 64), ["P0"], ["oL"], 2048.0 + 256 * XB)
        tt(sm("c"), pc(1, 0, 64), sm("e0"), ALU.is_lt, ["P1", "e0"], ["c"])
        tt(sm("m01"), pc(1, 0, 64), sm("e0"), ALU.min, ["P1", "e0"], ["m01"])
        tt(sm("t"), pc(3, 128, 64), sm("c"), ALU.mult, ["c", "P3"], ["t"])
        tt(sm("v"), sm("m01"), TH, ALU.is_lt, ["m01", "thT"], ["v"])
        tt(sm("dq"), pc(3, 448, 64), sm("t"), ALU.add, ["t", "P3"], ["dq"])
        tt(sm("mt"), sm("m01"), TH, ALU.min, ["m01", "thT"], ["mt"])
        tt(sm("t2"), sm("v"), sm("dq"), ALU.mult, ["v", "dq"], ["t2"])
        tt(sm("q01"), sm("t2"), tf(SI), ALU.add, ["t2", "tI"], ["q01"])
        tt(sm("u1"), pc(2, 0, 64), sm("mt"), ALU.is_lt, ["P2", "mt"], ["u1"])
        tt(sm("dbq"), pc(3, 0, 64), sm("q01"), ALU.subtract, ["P3", "q01"], ["dbq"])
        tt(sm("u2"), sm("u1"), sm("dbq"), ALU.mult, ["u1", "dbq"], ["u2"])
        tt(tf(SW), sm("u2"), sm("q01"), ALU.add, ["u2", "q01", "TT"], ["tW"])
        pieces(SW, "tW", 5)
        table("a", RW, 5, "d_t%d" % (2 + 3 * rnd))
        mm([back(4, 0, SW)], ["mG", "tW"], ["P4"])
        mask(0, "v")
        move("a", off(OW), pc(4, 0, 64), ["P4"], ["oW"], 2048.0)
        acc([(pc(0, 0, 256), NEG, tf(SN, 4)), (pc(0, 192, 64), NEG, tf(SV))], ["mK", "tNV", "tI", "TT"], 0, True)
        tt(T.GU[:], T.CH[:, 512:768].indirect(off(OL)), T.MK[:], ALU.mult, ["CH2", "oL", "MK0", "MK1"], ["GU"])
        mm([(pc(7, 0, 64), [(T.mO[:, 15 - r:143 - r], T.GU[:, r:1024:16]) for r in range(16)])], ["mO", "GU"], ["P7"])
        acc(turn(0, 64, 8, T.mT[:, 72:80], T.GU), ["mV", "GU"], 0)
        tt(sm("p01"), sm("t"), tf(SP), ALU.add, ["t", "tP"], ["p01"])
        tt(sm("u3"), pc(2, 0, 64), sm("m01"), ALU.is_lt, ["P2", "m01"], ["u3"])
        tt(sm("dbp"), pc(3, 0, 64), sm("p01"), ALU.subtract, ["P3", "p01"], ["dbp"])
        cols = [256 * d for d in (peers + [rank] if last else range(4))]
        for i in range(2):
            acc([(pc(SBANK[i], 0, 256), TWO, T.xo[:, cols[i]:cols[i] + 256])], ["mL"] + XO, SBANK[i], True)
        ts(off(OU), pc(7, 0, 64), 2048.0, ALU.add, ["P7"], ["oU"])
        act(T.GF[:], T.TB[:, 0:4096].indirect(off(OW)), TK + ["oW"], ["GF"])
        cp(T.GB[:], T.TB[:, 0:4096].indirect(off(OU)), TK + ["oU"], ["GB"])
        tt(sm("u4"), sm("u3"), sm("dbp"), ALU.mult, ["u3", "dbp"], ["u4"])
        tt(tf(SP), sm("u4"), sm("p01"), ALU.add, ["u4", "p01"], ["tP"])
        acc(turn(0, 0, 24, T.mT[:, 40:64], T.GF), ["mT", "GF"], 0)
        acc(turn(0, 192, 8, T.mT[:, 64:72], T.GB), ["mT", "GB"], 0, False, True)
        if not last:
            mm([back(6, 0, SP)], ["mG", "tP"], ["P6"])
            move("a", off(OP), pc(6, 0, 64), ["P6"], ["oP"], 2048.0)
        ts(sm("cc", 2), pc(0, 128, 128), 0.0, ALU.is_equal, ["P0"], ["cc"])
        tt(sm("ee", 2), pc(0, 0, 128), sm("cc", 2), ALU.mult, ["P0", "cc"], ["ee"])
        tt(tf(SN, 2), sm("ee", 2), tf(SN, 2), ALU.add, ["ee", "tNV"], ["tNV"])
        mm([back(4, 0, SV)], ["mG", "tNV"], ["P4"])
        mm([back(5, 0, SN), back(5, 64, SV)], ["mG", "tNV"], ["P5"])
        ts(off(OV), pc(4, 0, 64), 2048.0, ALU.add, ["P4"], ["oV"])
        move("a", off(ON), pc(5, 0, 64), ["P5"], ["oN"], 2048.0)

        def gathers(i):
            a, k = cols[i], SBANK[i]
            cp(T.G1[:, a:a + 256], X.indirect(off(OV, a // 16, a // 16 + 16)), XK[rnd] + ["oV"], ["G1_%d" % i])
            act(T.G2[:, a:a + 256], X.indirect(off(ON, a // 16, a // 16 + 16)), XK[rnd] + ["oN"], ["G2_%d" % i])

        def add_up(i):
            a, k = cols[i], SBANK[i]
            acc(([(pc(k, 0, 256), TWO, T.xo[:, a:a + 256])] if i > 1 else [])
                + [(pc(k, 0, 256), EYE, T.G1[:, a:a + 256]), (pc(k, 0, 256), EYE, T.G2[:, a:a + 256])],
                ["mI", "mL", "G1_%d" % i, "G2_%d" % i, XO[a // 256]], k, i > 1, True)

        def mean(i, e):
            a, k = cols[i], SBANK[i]
            if e == "v":
                ts(T.xo[:, a:a + 256], pc(k, 0, 256), 0.25, ALU.mult, ["P%d" % k], [XO[a // 256]], XB / 2 - 0.375, ALU.add)
            else:
                act(T.xo[:, a:a + 256], pc(k, 0, 256), ["P%d" % k], [XO[a // 256]], func=ACT.Identity, scale=0.25, bias=XB / 2 - 0.375)

        if not last:
            for step in SMOOTH.split():
                w, e, i = step[0].lower(), "v" if step[0].isupper() else "a", int(step[1:] or 0)
                if w == "g":
                    gathers(i)
                elif w == "s":
                    add_up(i)
                elif w == "p":
                    pieces((SV, SN)[i], "tNV", 6 + i)
                elif w == "f":
                    flags_sum()
                elif w == "c":
                    table(e, (RV, RN)[i], 6 + i, "d_t%d" % (3 + i + 3 * rnd))
                elif w == "x":
                    mean(i, e)
                elif w == "h":
                    high(5, 64)
                elif w == "b":
                    k = BBANK[i]
                    mm([(P[k][:, :, q, :], [(T.mB[:, 128 * q:128 * q + 128], T.xo[:, 128 * i:128 * i + 128])]) for q in range(4)],
                       ["mB", XO[i // 2]], ["P%d" % k])
                    move(e, XT[rnd + 1][:, 512 * i:512 * i + 512], pc(k, 0, 512), ["P%d" % k], [XK[rnd + 1][i]], -XB)
                elif w == "n":
                    n_gather(0)
                else:
                    n_turn()

    def home(n):
        d, k = (peers + [rank])[n], 4 + n
        mm([(P[k][:, 0:8, q, :], [(T.mF[:, 192 * q + 3 - j:192 * q + 131 - j], T.xo[:, 256 * d + 64 * j:256 * d + 64 * j + 64]) for j in range(4)])
            for q in range(4)], ["mF", XO[d]], ["P%d" % k])

    def leave(n, e):
        d, k = (peers + [rank])[n], 4 + n
        if d == rank:
            move(e, T.ox[:, d, :], pc(k, 0, 256), ["P%d" % k], ["ox%d" % d], -XB)
            dmas("s", "d_out", [(T.yx[32 * d:32 * d + 32, :], T.ox[:, d, :])], ["ox%d" % d], [])
        else:
            move(e, T.sx[:, d, 0:256], pc(k, 0, 256), ["P%d" % k], ["sx%d" % d])
            w = 256 if n == 2 else 304
            send(3, d, T.lx[:, rank, 0:w], T.sx[:, d, 0:w], ["sy", "sx%d" % d], "lx%d" % d)

    gathers(0)
    LB = (3, 6, 7, 0)
    for d in range(4):
        mm([(P[LB[d]][:, t, 0:2, :],
             [(T.mZ[32 * d:32 * d + 32, 65 + 64 * d - 64 * s - j:193 + 64 * d - 64 * s - j],
               T.TT[32 * d:32 * d + 32, 16 * slot + 1 + 8 * s + 4 * j:16 * slot + 5 + 8 * s + 4 * j:2, :]) for s in range(2) for j in range(2)])
            for t, slot in enumerate((SN, SV, SP))], ["mZ", "tNV", "tP"], ["P%d" % LB[d]])
    add_up(0)
    gathers(1)
    for d in range(4):
        move("a", T.sx[:, d, 256:304], P[LB[d]][:, 0:3, 0:2, :], ["P%d" % LB[d]], ["sy"])
    mean(0, "v")
    add_up(1)
    home(0)
    send(2, peers[2], T.lx[:, rank, 256:304], T.sx[:, peers[2], 256:304], ["sy"], "ly%d" % peers[2])
    gathers(2)
    leave(0, "v")
    mean(1, "a")
    add_up(2)
    home(1)
    gathers(3)
    leave(1, "a")
    mean(2, "v")
    add_up(3)
    home(2)
    leave(2, "v")
    mean(3, "a")
    home(3)
    leave(3, "a")
    ts(T.col[:, 4:5], T.pi[:, 0:1], 64.0, ALU.is_lt, ["pi0"], ["ms"])
    ts(T.col[:, 5:6], T.pi[:, 0:1], 64.0, ALU.is_ge, ["pi0"], ["ms"])

    def halves(d, src, key):
        for s in range(2):
            ts(T.lf[:, :, d, s, :], src[:, d, 256:304], T.col[:, 4 + s:5 + s], ALU.mult, ["ms", key], ["lf"])

    halves(rank, T.sx, "sy")
    halves(peers[2], T.lx, "ly%d" % peers[2])
    for n, d in enumerate(peers):
        move("av"[n // 2], T.ox[:, d, :], T.lx[:, d, 0:256], ["lx%d" % d], ["ox%d" % d], -XB)
        dmas("s", "d_out", [(T.yx[32 * d:32 * d + 32, :], T.ox[:, d, :])], ["ox%d" % d], [])
        if n < 2:
            halves(d, T.lx, "lx%d" % d)
        if n == 1:
            mm([(pc(0, 64 * t, 64), [(T.lf[:, t, :, :, :], T.mJ[:])]) for t in range(3)], ["mJ", "lf"], ["P0"])
            move("a", T.yl[:], pc(0, 0, 192), ["P0"], ["yl"], 2048.0)
            dmas("a", "d_out", [(T.yn[:], T.yl[:, 0:64]), (T.yv[:], T.yl[:, 64:128]), (T.yp[:], T.yl[:, 128:192])], ["yl"], [])
    for s, v in total.items():
        g.wait_ge(T.sem[s], v)
